import numpy as np
import ml_dtypes


def mxq(x, axis, fmt="e4m3"):
    dtype, down = {"e4m3": (ml_dtypes.float8_e4m3fn, 7), "e5m2": (ml_dtypes.float8_e5m2, 14)}[fmt]
    v = np.moveaxis(np.asarray(x, np.float32).astype(ml_dtypes.bfloat16).astype(np.float64), axis, -1)
    blocks = v.reshape(v.shape[:-1] + (-1, 32))
    amax = np.abs(blocks).max(-1, keepdims=True)
    byte = np.maximum(np.where(amax > 0, np.frexp(amax)[1] - 1 + 127, 0) - down, 1)
    scale = np.exp2(byte - 127.0)
    codes = (blocks / scale).astype(np.float32).astype(dtype).astype(np.float64)
    return np.moveaxis((codes * scale).reshape(v.shape), -1, axis)


WIDE = False


def mx_kscale(k):
    if not WIDE:
        return np.ones(k)
    levels = np.array([10, -10, 5, -5, 0])
    if k % 512:
        return np.exp2(np.random.permutation(np.resize(levels, k // 32))).repeat(32)
    a = np.empty((k // 512, 16))
    for p in range(k // 512):
        a[p, :8] = np.random.permutation(np.resize(levels, 8))
        for g in range(8):
            far = levels[np.abs(levels - a[p, g]) >= 10]
            a[p, g + 8] = far[np.random.randint(len(far))]
    return np.exp2(a.ravel()).repeat(32)


def f64(x):
    return np.asarray(x).astype(np.float64)


def striped(idx):
    return np.tile(idx.reshape(-1, 16).T, (8, 1)).astype(np.uint16)


def unstriped(offs):
    return offs[:16].T.reshape(-1).astype(np.int64)


def gelu(v):
    return 0.5 * v * (1.0 + np.tanh(np.sqrt(2.0 / np.pi) * (v + 0.044715 * v**3)))


K, T, E, C, H, N = 1024, 512, 8, 128, 512, 256


def by_expert(wq, xq):
    return np.concatenate([wq[e].T @ xq[:, e * C:(e + 1) * C] for e in range(E)], axis=1)


def setup_inputs():
    n = np.random.standard_normal
    s = mx_kscale(K)[:, None]
    u = mx_kscale(H)
    first = np.random.permutation(np.repeat(np.arange(E), T // E))
    second = (first + 1 + np.random.permutation(np.repeat(np.arange(E - 1), -(-T // (E - 1)))[:T])) % E
    while np.bincount(second, minlength=E).max() != T // E:
        load = np.bincount(second, minlength=E); hi, lo = int(load.argmax()), int(load.argmin())
        t = np.flatnonzero((second == hi) & (first != lo))[0]; second[t] = lo
    slot_token = np.empty(E * C, np.int64); pos = np.empty((2, T), np.int64); fill = np.zeros(E, np.int64)
    place = np.stack([np.random.permutation(C) for _ in range(E)])
    for r, deal in enumerate((first, second)):
        for t in np.random.permutation(T):
            e = deal[t]; j = e * C + place[e, fill[e]]; fill[e] += 1; slot_token[j] = t; pos[r, t] = j
    g = np.random.uniform(0.2, 0.8, T)
    return {
        "xT": (n((K, T)) * s).astype(np.float32),
        "w1": (n((E, K, H)) / np.sqrt(K) / s[None]).astype(np.float32),
        "w3": (n((E, K, H)) / np.sqrt(K) / s[None] * u[None, None, :]).astype(np.float32),
        "w2": (n((E, H, N)) / np.sqrt(H) / u[None, :, None]).astype(np.float32),
        "gate": np.stack([np.tile(g, (N, 1)), np.tile(1.0 - g, (N, 1))]).astype(np.float32),
        "offs": striped(slot_token),
        "pos1": striped(pos[0]),
        "pos2": striped(pos[1]),
    }


def reference(xT, w1, w3, w2, gate, offs, pos1, pos2):
    idx = unstriped(offs)
    xq = mxq(f64(xT)[:, idx], 0, "e4m3")
    h = gelu(by_expert(mxq(f64(w1), 1, "e4m3"), xq))
    h = h * by_expert(mxq(f64(w3), 1, "e4m3"), xq)
    y = by_expert(mxq(f64(w2), 1, "e4m3"), mxq(h, 0, "e4m3"))
    return f64(gate[0]) * y[:, unstriped(pos1)] + f64(gate[1]) * y[:, unstriped(pos2)]

@@ -1,0 +1,293 @@
+from contextlib import ExitStack
+
+import concourse.mybir as mybir
+
+K, T, E, C, H, N = 1024, 512, 8, 128, 512, 256
+FLOPS = 2 * E * C * (2 * K * H + H * N)
+
+F32 = mybir.dt.float32
+BF16 = mybir.dt.bfloat16
+U32 = mybir.dt.uint32
+U16 = mybir.dt.uint16
+U8 = mybir.dt.uint8
+FP8X4 = mybir.dt.float8_e4m3fn_x4
+GELU = mybir.ActivationFunctionType.Gelu_apprx_tanh
+MULT = mybir.AluOpType.mult
+ADD = mybir.AluOpType.add
+
+P = 128
+PACK = 4
+K_PASS = P * PACK
+PASSES = K // K_PASS
+SLICE = 256
+SLICES = E * C // SLICE
+NB = N // P
+RAW_BUFS = 10
+GRP_BUFS = 6
+LAG = 3
+TILES_A_PAIR = 9
+N_TILES = TILES_A_PAIR * E // 2
+TAIL_TILES = 3
+X_ROUND = "V"
+
+
+def scalar_share(i):
+    if i >= N_TILES - TAIL_TILES:
+        return 44
+    if i % TILES_A_PAIR == 8:
+        return 0
+    return 0 if i % 3 == 2 else 128
+
+
+def tile_routed_moe_kernel(tc, xT, w1, w3, w2, gate, offs, pos1, pos2, out):
+    nc = tc.nc
+    with ExitStack() as ctx:
+        lists = ctx.enter_context(tc.tile_pool(name="lists", bufs=1))
+        keep = ctx.enter_context(tc.tile_pool(name="keep", bufs=1))
+        raws = ctx.enter_context(tc.tile_pool(name="raws", bufs=RAW_BUFS))
+        stage = ctx.enter_context(tc.tile_pool(name="stage", bufs=GRP_BUFS))
+        codes = ctx.enter_context(tc.tile_pool(name="codes", bufs=3))
+        hid = ctx.enter_context(tc.tile_pool(name="hid", bufs=2))
+        psum = ctx.enter_context(tc.psum_pool(name="psum", bufs=2))
+
+        offs_t = lists.tile([P, E * C // 16], U16, name="offs_t")
+        pos1_t = lists.tile([P, T // 16], U16, name="pos1_t")
+        pos2_t = lists.tile([P, T // 16], U16, name="pos2_t")
+        nc.sync.dma_start(offs_t[:], offs)
+
+        warm = keep.tile([P, 1], F32, name="warm")
+        warm_out = keep.tile([P, 1], F32, name="warm_out")
+        nc.vector.memset(warm[:], 0.0)
+        nc.scalar.activation(out=warm_out[:], in_=warm[:], func=GELU)
+
+        x_view = xT.rearrange("(g p t) n -> g p t n", p=P, t=PACK)
+        planes = []
+        for g in range(PASSES):
+            row = []
+            for t in range(PACK):
+                plane = keep.tile([P, T], F32, name="plane%d%d" % (g, t))
+                nc.sync.dma_start(plane[:], x_view[g, :, t, :])
+                row.append(plane)
+            planes.append(row)
+
+        x_codes = keep.tile([P, PASSES, E * C], U32, name="x_codes", align_bytes=64)
+        x_scales = keep.tile([P, PASSES, E * C], U8, name="x_scales", align_bytes=64)
+        h_codes = keep.tile([P, E, C], U32, name="h_codes", align_bytes=64)
+        h_scales = keep.tile([P, E, C], U8, name="h_scales", align_bytes=64)
+        y_tiles = [keep.tile([P, E * C], F32, name="y%d" % nb) for nb in range(NB)]
+        gate_tiles = [[keep.tile([P, T], F32, name="gate%d%d" % (r, nb)) for nb in range(NB)] for r in range(2)]
+
+        gathered = {}
+        rounded = {}
+
+        def gather(s, g, t):
+            if t == 0:
+                gathered[(s, g)] = stage.tile([P, PACK, SLICE], F32, name="g4", bufs=2)
+            nc.vector.tensor_copy(
+                gathered[(s, g)][:, t, :],
+                planes[g][t][:].indirect(offs_t[:, s * SLICE // 16 : (s + 1) * SLICE // 16]),
+            )
+
+        def round_x(s, g):
+            xb = stage.tile([P, SLICE, PACK], BF16, name="xb", bufs=2, align_bytes=64)
+            src = gathered[(s, g)][:].rearrange("p t n -> p n t")
+            if X_ROUND == "S":
+                nc.scalar.copy(out=xb[:], in_=src)
+            else:
+                nc.vector.tensor_copy(out=xb[:], in_=src)
+            rounded[(s, g)] = xb
+
+        def quantize_x(s, g):
+            cols = slice(s * SLICE, (s + 1) * SLICE)
+            nc.vector.quantize_mx(
+                out=x_codes[:, g, cols].bitcast(FP8X4),
+                scales=x_scales[:, g, cols],
+                in_=rounded[(s, g)][:].rearrange("p n t -> p (n t)"),
+            )
+
+        def tile_info(i):
+            a, k = divmod(i, TILES_A_PAIR)
+            if k == 8:
+                return ("w2", a, 0)
+            return (("w1", "w3")[k % 2], 2 * a + k // 4, (k % 4) // 2)
+
+        w_codes = {}
+        w_scales = {}
+        grouped = {}
+
+        def split_copy(dst_s, src_s, dst_v, src_v, share, groups, v_cols_a_group):
+            if share > 0:
+                nc.scalar.copy(out=dst_s[:, 0:share], in_=src_s[:, 0:share])
+            if share < groups:
+                nc.vector.tensor_copy(out=dst_v[:, share * v_cols_a_group :], in_=src_v[:, share * v_cols_a_group :])
+
+        def load_and_interleave(i):
+            kind, e, g = tile_info(i)
+            raw = raws.tile([P, PACK * H], F32, name="raw")
+            grp = stage.tile([P, PACK * H], BF16, name="grp", align_bytes=64)
+            share = scalar_share(i)
+            if kind == "w2":
+                nc.sync.dma_start(
+                    out=raw[:].rearrange("p (e r) -> p e r", e=2),
+                    in_=w2[2 * e : 2 * e + 2].rearrange("e (p j) n -> p e (j n)", j=PACK),
+                )
+                for half in range(2):
+                    r = raw[:, half * PACK * N : (half + 1) * PACK * N]
+                    d = grp[:, half * PACK * N : (half + 1) * PACK * N]
+                    split_copy(
+                        d.rearrange("p (c i j) -> p c j i", i=4, j=PACK),
+                        r.rearrange("p (j c i) -> p c j i", j=PACK, i=4),
+                        d.rearrange("p (c j) -> p c j", j=PACK),
+                        r.rearrange("p (j c) -> p c j", j=PACK),
+                        share * (N // 4) // 128,
+                        N // 4,
+                        4,
+                    )
+            else:
+                src = w1 if kind == "w1" else w3
+                nc.sync.dma_start(
+                    out=raw[:].rearrange("p (j c) -> p j c", j=PACK),
+                    in_=src[e, g * K_PASS : (g + 1) * K_PASS, :].rearrange("(p j) c -> p j c", j=PACK),
+                )
+                split_copy(
+                    grp[:].rearrange("p (t m j) -> p m j t", t=4, j=PACK),
+                    raw[:].rearrange("p (j m t) -> p m j t", j=PACK, t=4),
+                    grp[:].rearrange("p (t m j) -> p m t j", t=4, j=PACK),
+                    raw[:].rearrange("p (j m t) -> p m t j", j=PACK, t=4),
+                    share,
+                    128,
+                    1,
+                )
+            grouped[i] = grp
+
+        def quantize_w(i):
+            kind, e, g = tile_info(i)
+            if g == 0:
+                passes = 1 if kind == "w2" else PASSES
+                w_codes[(kind, e)] = codes.tile([P, passes, H], U32, name=kind + "c", align_bytes=64)
+                w_scales[(kind, e)] = codes.tile([P, passes, H], U8, name=kind + "s", align_bytes=64)
+            nc.vector.quantize_mx(
+                out=w_codes[(kind, e)][:, g, :].bitcast(FP8X4),
+                scales=w_scales[(kind, e)][:, g, :],
+                in_=grouped[i][:],
+            )
+
+        banks = {}
+        hidden = {}
+
+        def layer1(e):
+            slots = slice(e * C, (e + 1) * C)
+            for kind in ("w1", "w3"):
+                bank = psum.tile([P, PACK, C], F32, name="bank_" + kind)
+                for t in range(PACK):
+                    for g in range(PASSES):
+                        nc.tensor.matmul_mx(
+                            out=bank[:, t, :],
+                            lhsT=w_codes[(kind, e)][:, g, t * P : (t + 1) * P].bitcast(FP8X4),
+                            lhsT_scale=w_scales[(kind, e)][:, g, t * P : (t + 1) * P],
+                            rhs=x_codes[:, g, slots].bitcast(FP8X4),
+                            rhs_scale=x_scales[:, g, slots],
+                            start=(g == 0),
+                            stop=(g == PASSES - 1),
+                        )
+                banks[(kind, e)] = bank
+                if kind == "w1":
+                    act = hid.tile([P, PACK, C], F32, name="act")
+                    nc.scalar.activation(out=act[:], in_=bank[:], func=GELU)
+                    hidden[e] = act
+
+        def gate_hidden(e):
+            hb = hid.tile([P, C, PACK], BF16, name="hb", align_bytes=64)
+            nc.vector.tensor_tensor(
+                hb[:],
+                hidden[e][:].rearrange("p t n -> p n t"),
+                banks[("w3", e)][:].rearrange("p t n -> p n t"),
+                MULT,
+            )
+            hidden[e] = hb
+
+        def quantize_hidden(e):
+            nc.vector.quantize_mx(
+                out=h_codes[:, e, :].bitcast(FP8X4),
+                scales=h_scales[:, e, :],
+                in_=hidden[e][:].rearrange("p n t -> p (n t)"),
+            )
+
+        def layer2(a):
+            bank = psum.tile([P, NB, 2, C], F32, name="bank_y")
+            for nb in range(NB):
+                for half in range(2):
+                    cols = slice(half * N + nb * P, half * N + (nb + 1) * P)
+                    nc.tensor.matmul_mx(
+                        out=bank[:, nb, half, :],
+                        lhsT=w_codes[("w2", a)][:, 0, cols].bitcast(FP8X4),
+                        lhsT_scale=w_scales[("w2", a)][:, 0, cols],
+                        rhs=h_codes[:, 2 * a + half, :].bitcast(FP8X4),
+                        rhs_scale=h_scales[:, 2 * a + half, :],
+                        start=True,
+                        stop=True,
+                    )
+                nc.scalar.copy(
+                    out=y_tiles[nb][:, 2 * a * C : (2 * a + 2) * C],
+                    in_=bank[:, nb, :, :].rearrange("p h c -> p (h c)"),
+                )
+
+        for g in range(PASSES):
+            for t in range(PACK):
+                gather(0, g, t)
+        round_x(0, 0)
+        round_x(0, 1)
+        quantize_x(0, 0)
+        quantize_x(0, 1)
+
+        later = {}
+
+        def defer(step, fn, arg):
+            later.setdefault(step, []).append((fn, arg))
+
+        done = 0
+        for i in range(N_TILES + 6):
+            if i < N_TILES:
+                load_and_interleave(i)
+                if i == 5:
+                    nc.sync.dma_start(pos1_t[:], pos1)
+                    nc.sync.dma_start(pos2_t[:], pos2)
+                s = i // TILES_A_PAIR + 1
+                k = i % TILES_A_PAIR
+                if s < SLICES:
+                    if k < 8:
+                        gather(s, k // PACK, k % PACK)
+                    if k == 5:
+                        round_x(s, 0)
+                    if k == 6:
+                        quantize_x(s, 0)
+                    if k == 8:
+                        round_x(s, 1)
+                if 2 <= s <= SLICES and k == 0:
+                    quantize_x(s - 1, 1)
+            lag = min(LAG, max(0, N_TILES - 1 - i))
+            while done < N_TILES and done <= i - lag:
+                quantize_w(done)
+                kind, e, g = tile_info(done)
+                if kind == "w3" and g == 1:
+                    defer(i, layer1, e)
+                    defer(i + 1, gate_hidden, e)
+                    defer(i + 2, quantize_hidden, e)
+                if kind == "w2":
+                    defer(i + 2, layer2, e)
+                done += 1
+            for fn, arg in later.get(i, []):
+                fn(arg)
+
+        for nb in range(NB):
+            for r in range(2):
+                nc.sync.dma_start(gate_tiles[r][nb][:], gate[r, nb * P : (nb + 1) * P, :])
+
+        for nb in range(NB):
+            first = hid.tile([P, T], F32, name="first")
+            second = hid.tile([P, T], F32, name="second")
+            nc.vector.tensor_tensor(first[:], y_tiles[nb][:].indirect(pos1_t[:]), gate_tiles[0][nb][:], MULT)
+            nc.vector.tensor_tensor(second[:], y_tiles[nb][:].indirect(pos2_t[:]), gate_tiles[1][nb][:], MULT)
+            total = hid.tile([P, T], F32, name="total")
+            nc.vector.tensor_tensor(total[:], first[:], second[:], ADD)
+            nc.sync.dma_start(out[nb * P : (nb + 1) * P, :], total[:])

@@ -1,6 +1,7 @@
 from contextlib import ExitStack
 
 import concourse.mybir as mybir
+from concourse.masks import make_identity
 
 K, T, E, C, H, N = 1024, 512, 8, 128, 512, 256
 FLOPS = 2 * E * C * (2 * K * H + H * N)
@@ -25,17 +26,16 @@ NB = N // P
 RAW_BUFS = 10
 GRP_BUFS = 6
 LAG = 3
-TILES_A_PAIR = 9
-N_TILES = TILES_A_PAIR * E // 2
-TAIL_TILES = 3
+BIG_TILES = 4 * E
+W2_GROUPS = [(0, 2), (2, 2), (4, 2), (6, 1), (7, 1)]
+N_TILES = BIG_TILES + len(W2_GROUPS)
 X_ROUND = "V"
+W2_SHARE = 44
 
 
 def scalar_share(i):
-    if i >= N_TILES - TAIL_TILES:
-        return 44
-    if i % TILES_A_PAIR == 8:
-        return 0
+    if i >= BIG_TILES:
+        return W2_SHARE
     return 0 if i % 3 == 2 else 128
 
 
@@ -59,6 +59,9 @@ def tile_routed_moe_kernel(tc, xT, w1, w3, w2, gate, offs, pos1, pos2, out):
         warm_out = keep.tile([P, 1], F32, name="warm_out")
         nc.vector.memset(warm[:], 0.0)
         nc.scalar.activation(out=warm_out[:], in_=warm[:], func=GELU)
+
+        ident = keep.tile([P, P], F32, name="ident")
+        make_identity(nc, ident[:])
 
         x_view = xT.rearrange("(g p t) n -> g p t n", p=P, t=PACK)
         planes = []
@@ -106,10 +109,9 @@ def tile_routed_moe_kernel(tc, xT, w1, w3, w2, gate, offs, pos1, pos2, out):
             )
 
         def tile_info(i):
-            a, k = divmod(i, TILES_A_PAIR)
-            if k == 8:
-                return ("w2", a, 0)
-            return (("w1", "w3")[k % 2], 2 * a + k // 4, (k % 4) // 2)
+            if i >= BIG_TILES:
+                return ("w2", i - BIG_TILES, 0)
+            return (("w1", "w3")[i % 2], i // 4, (i % 4) // 2)
 
         w_codes = {}
         w_scales = {}
@@ -127,21 +129,22 @@ def tile_routed_moe_kernel(tc, xT, w1, w3, w2, gate, offs, pos1, pos2, out):
             grp = stage.tile([P, PACK * H], BF16, name="grp", align_bytes=64)
             share = scalar_share(i)
             if kind == "w2":
+                e0, count = W2_GROUPS[e]
                 nc.sync.dma_start(
-                    out=raw[:].rearrange("p (e r) -> p e r", e=2),
-                    in_=w2[2 * e : 2 * e + 2].rearrange("e (p j) n -> p e (j n)", j=PACK),
+                    out=raw[:, 0 : count * PACK * N].rearrange("p (e r) -> p e r", e=count),
+                    in_=w2[e0 : e0 + count].rearrange("e (p j) n -> p e (j n)", j=PACK),
                 )
-                for half in range(2):
+                for half in range(count):
                     r = raw[:, half * PACK * N : (half + 1) * PACK * N]
                     d = grp[:, half * PACK * N : (half + 1) * PACK * N]
                     split_copy(
-                        d.rearrange("p (c i j) -> p c j i", i=4, j=PACK),
-                        r.rearrange("p (j c i) -> p c j i", j=PACK, i=4),
                         d.rearrange("p (c j) -> p c j", j=PACK),
                         r.rearrange("p (j c) -> p c j", j=PACK),
-                        share * (N // 4) // 128,
-                        N // 4,
-                        4,
+                        d.rearrange("p (c j) -> p c j", j=PACK),
+                        r.rearrange("p (j c) -> p c j", j=PACK),
+                        share * N // 128,
+                        N,
+                        1,
                     )
             else:
                 src = w1 if kind == "w1" else w3
@@ -150,12 +153,12 @@ def tile_routed_moe_kernel(tc, xT, w1, w3, w2, gate, offs, pos1, pos2, out):
                     in_=src[e, g * K_PASS : (g + 1) * K_PASS, :].rearrange("(p j) c -> p j c", j=PACK),
                 )
                 split_copy(
-                    grp[:].rearrange("p (t m j) -> p m j t", t=4, j=PACK),
-                    raw[:].rearrange("p (j m t) -> p m j t", j=PACK, t=4),
-                    grp[:].rearrange("p (t m j) -> p m t j", t=4, j=PACK),
-                    raw[:].rearrange("p (j m t) -> p m t j", j=PACK, t=4),
-                    share,
-                    128,
+                    grp[:].rearrange("p (c j) -> p c j", j=PACK),
+                    raw[:].rearrange("p (j c) -> p c j", j=PACK),
+                    grp[:].rearrange("p (c j) -> p c j", j=PACK),
+                    raw[:].rearrange("p (j c) -> p c j", j=PACK),
+                    share * H // 128,
+                    H,
                     1,
                 )
             grouped[i] = grp
@@ -166,10 +169,11 @@ def tile_routed_moe_kernel(tc, xT, w1, w3, w2, gate, offs, pos1, pos2, out):
                 passes = 1 if kind == "w2" else PASSES
                 w_codes[(kind, e)] = codes.tile([P, passes, H], U32, name=kind + "c", align_bytes=64)
                 w_scales[(kind, e)] = codes.tile([P, passes, H], U8, name=kind + "s", align_bytes=64)
+            width = W2_GROUPS[e][1] * N if kind == "w2" else H
             nc.vector.quantize_mx(
-                out=w_codes[(kind, e)][:, g, :].bitcast(FP8X4),
-                scales=w_scales[(kind, e)][:, g, :],
-                in_=grouped[i][:],
+                out=w_codes[(kind, e)][:, g, 0:width].bitcast(FP8X4),
+                scales=w_scales[(kind, e)][:, g, 0:width],
+                in_=grouped[i][:, 0 : PACK * width],
             )
 
         banks = {}
@@ -178,32 +182,35 @@ def tile_routed_moe_kernel(tc, xT, w1, w3, w2, gate, offs, pos1, pos2, out):
         def layer1(e):
             slots = slice(e * C, (e + 1) * C)
             for kind in ("w1", "w3"):
-                bank = psum.tile([P, PACK, C], F32, name="bank_" + kind)
-                for t in range(PACK):
-                    for g in range(PASSES):
-                        nc.tensor.matmul_mx(
-                            out=bank[:, t, :],
-                            lhsT=w_codes[(kind, e)][:, g, t * P : (t + 1) * P].bitcast(FP8X4),
-                            lhsT_scale=w_scales[(kind, e)][:, g, t * P : (t + 1) * P],
-                            rhs=x_codes[:, g, slots].bitcast(FP8X4),
-                            rhs_scale=x_scales[:, g, slots],
-                            start=(g == 0),
-                            stop=(g == PASSES - 1),
-                        )
+                bank = psum.tile([P, H], F32, name="bank_" + kind)
+                for g in range(PASSES):
+                    nc.tensor.matmul_mx(
+                        out=bank[:],
+                        lhsT=x_codes[:, g, slots].bitcast(FP8X4),
+                        lhsT_scale=x_scales[:, g, slots],
+                        rhs=w_codes[(kind, e)][:, g, :].bitcast(FP8X4),
+                        rhs_scale=w_scales[(kind, e)][:, g, :],
+                        start=(g == 0),
+                        stop=(g == PASSES - 1),
+                    )
                 banks[(kind, e)] = bank
                 if kind == "w1":
-                    act = hid.tile([P, PACK, C], F32, name="act")
+                    act = hid.tile([P, H], F32, name="act")
                     nc.scalar.activation(out=act[:], in_=bank[:], func=GELU)
                     hidden[e] = act
 
         def gate_hidden(e):
+            h_rows = hid.tile([P, H], BF16, name="h_rows")
+            nc.vector.tensor_tensor(h_rows[:], hidden[e][:], banks[("w3", e)][:], MULT)
+            hidden[e] = h_rows
+
+        def turn_hidden(e):
+            words = hidden[e][:].bitcast(F32)
+            turned = psum.tile([P, 2, C], F32, name="turned")
+            for u in range(2):
+                nc.tensor.transpose(turned[:, u, :], words[:, u : H // 2 : 2], ident[:])
             hb = hid.tile([P, C, PACK], BF16, name="hb", align_bytes=64)
-            nc.vector.tensor_tensor(
-                hb[:],
-                hidden[e][:].rearrange("p t n -> p n t"),
-                banks[("w3", e)][:].rearrange("p t n -> p n t"),
-                MULT,
-            )
+            nc.scalar.copy(out=hb[:].bitcast(F32), in_=turned[:].rearrange("p u n -> p n u"))
             hidden[e] = hb
 
         def quantize_hidden(e):
@@ -214,22 +221,23 @@ def tile_routed_moe_kernel(tc, xT, w1, w3, w2, gate, offs, pos1, pos2, out):
             )
 
         def layer2(a):
+            e0, count = W2_GROUPS[a]
             bank = psum.tile([P, NB, 2, C], F32, name="bank_y")
             for nb in range(NB):
-                for half in range(2):
+                for half in range(count):
                     cols = slice(half * N + nb * P, half * N + (nb + 1) * P)
                     nc.tensor.matmul_mx(
                         out=bank[:, nb, half, :],
                         lhsT=w_codes[("w2", a)][:, 0, cols].bitcast(FP8X4),
                         lhsT_scale=w_scales[("w2", a)][:, 0, cols],
-                        rhs=h_codes[:, 2 * a + half, :].bitcast(FP8X4),
-                        rhs_scale=h_scales[:, 2 * a + half, :],
+                        rhs=h_codes[:, e0 + half, :].bitcast(FP8X4),
+                        rhs_scale=h_scales[:, e0 + half, :],
                         start=True,
                         stop=True,
                     )
                 nc.scalar.copy(
-                    out=y_tiles[nb][:, 2 * a * C : (2 * a + 2) * C],
-                    in_=bank[:, nb, :, :].rearrange("p h c -> p (h c)"),
+                    out=y_tiles[nb][:, e0 * C : (e0 + count) * C],
+                    in_=bank[:, nb, 0:count, :].rearrange("p h c -> p (h c)"),
                 )
 
         for g in range(PASSES):
@@ -252,18 +260,17 @@ def tile_routed_moe_kernel(tc, xT, w1, w3, w2, gate, offs, pos1, pos2, out):
                 if i == 5:
                     nc.sync.dma_start(pos1_t[:], pos1)
                     nc.sync.dma_start(pos2_t[:], pos2)
-                s = i // TILES_A_PAIR + 1
-                k = i % TILES_A_PAIR
+                s = i // 8 + 1
+                k = i % 8
                 if s < SLICES:
-                    if k < 8:
-                        gather(s, k // PACK, k % PACK)
+                    gather(s, k // PACK, k % PACK)
                     if k == 5:
                         round_x(s, 0)
                     if k == 6:
                         quantize_x(s, 0)
-                    if k == 8:
-                        round_x(s, 1)
                 if 2 <= s <= SLICES and k == 0:
+                    round_x(s - 1, 1)
+                if 2 <= s <= SLICES and k == 1:
                     quantize_x(s - 1, 1)
             lag = min(LAG, max(0, N_TILES - 1 - i))
             while done < N_TILES and done <= i - lag:
@@ -272,9 +279,10 @@ def tile_routed_moe_kernel(tc, xT, w1, w3, w2, gate, offs, pos1, pos2, out):
                 if kind == "w3" and g == 1:
                     defer(i, layer1, e)
                     defer(i + 1, gate_hidden, e)
+                    defer(i + 1, turn_hidden, e)
                     defer(i + 2, quantize_hidden, e)
                 if kind == "w2":
-                    defer(i + 2, layer2, e)
+                    defer(i, layer2, e)
                 done += 1
             for fn, arg in later.get(i, []):
                 fn(arg)

@@ -1,7 +1,6 @@
 from contextlib import ExitStack
 
 import concourse.mybir as mybir
-from concourse.masks import make_identity
 
 K, T, E, C, H, N = 1024, 512, 8, 128, 512, 256
 FLOPS = 2 * E * C * (2 * K * H + H * N)
@@ -23,20 +22,15 @@ PASSES = K // K_PASS
 SLICE = 256
 SLICES = E * C // SLICE
 NB = N // P
+TILE = PACK * H
 RAW_BUFS = 10
-GRP_BUFS = 6
-LAG = 3
+GRP_BUFS = 4
+LAG = 2
 BIG_TILES = 4 * E
-W2_GROUPS = [(0, 2), (2, 2), (4, 2), (6, 1), (7, 1)]
-N_TILES = BIG_TILES + len(W2_GROUPS)
-X_ROUND = "V"
-W2_SHARE = 44
-
-
-def scalar_share(i):
-    if i >= BIG_TILES:
-        return W2_SHARE
-    return 0 if i % 3 == 2 else 128
+W2_GROUPS = [(0, 4), (4, 2), (6, 1), (7, 1)]
+W2_TILES = [(0, 2), (2, 2), (4, 2), (6, 1), (7, 1)]
+N_TILES = BIG_TILES + len(W2_TILES)
+W2_SCALAR_COLS = 88
 
 
 def tile_routed_moe_kernel(tc, xT, w1, w3, w2, gate, offs, pos1, pos2, out):
@@ -46,7 +40,7 @@ def tile_routed_moe_kernel(tc, xT, w1, w3, w2, gate, offs, pos1, pos2, out):
         keep = ctx.enter_context(tc.tile_pool(name="keep", bufs=1))
         raws = ctx.enter_context(tc.tile_pool(name="raws", bufs=RAW_BUFS))
         stage = ctx.enter_context(tc.tile_pool(name="stage", bufs=GRP_BUFS))
-        codes = ctx.enter_context(tc.tile_pool(name="codes", bufs=3))
+        codes = ctx.enter_context(tc.tile_pool(name="codes", bufs=2))
         hid = ctx.enter_context(tc.tile_pool(name="hid", bufs=2))
         psum = ctx.enter_context(tc.psum_pool(name="psum", bufs=2))
 
@@ -60,9 +54,6 @@ def tile_routed_moe_kernel(tc, xT, w1, w3, w2, gate, offs, pos1, pos2, out):
         nc.vector.memset(warm[:], 0.0)
         nc.scalar.activation(out=warm_out[:], in_=warm[:], func=GELU)
 
-        ident = keep.tile([P, P], F32, name="ident")
-        make_identity(nc, ident[:])
-
         x_view = xT.rearrange("(g p t) n -> g p t n", p=P, t=PACK)
         planes = []
         for g in range(PASSES):
@@ -73,10 +64,11 @@ def tile_routed_moe_kernel(tc, xT, w1, w3, w2, gate, offs, pos1, pos2, out):
                 row.append(plane)
             planes.append(row)
 
-        x_codes = keep.tile([P, PASSES, E * C], U32, name="x_codes", align_bytes=64)
-        x_scales = keep.tile([P, PASSES, E * C], U8, name="x_scales", align_bytes=64)
+        x_codes = keep.tile([P, SLICES, PASSES, SLICE], U32, name="x_codes", align_bytes=64)
+        x_scales = keep.tile([P, SLICES, PASSES, SLICE], U8, name="x_scales", align_bytes=64)
         h_codes = keep.tile([P, E, C], U32, name="h_codes", align_bytes=64)
         h_scales = keep.tile([P, E, C], U8, name="h_scales", align_bytes=64)
+        h_bf = keep.tile([P, E, C, PACK], BF16, name="h_bf", align_bytes=64)
         y_tiles = [keep.tile([P, E * C], F32, name="y%d" % nb) for nb in range(NB)]
         gate_tiles = [[keep.tile([P, T], F32, name="gate%d%d" % (r, nb)) for nb in range(NB)] for r in range(2)]
 
@@ -84,28 +76,23 @@ def tile_routed_moe_kernel(tc, xT, w1, w3, w2, gate, offs, pos1, pos2, out):
         rounded = {}
 
         def gather(s, g, t):
-            if t == 0:
-                gathered[(s, g)] = stage.tile([P, PACK, SLICE], F32, name="g4", bufs=2)
+            if g == 0 and t == 0:
+                gathered[s] = stage.tile([P, PASSES, PACK, SLICE], F32, name="g4", bufs=1)
             nc.vector.tensor_copy(
-                gathered[(s, g)][:, t, :],
+                gathered[s][:, g, t, :],
                 planes[g][t][:].indirect(offs_t[:, s * SLICE // 16 : (s + 1) * SLICE // 16]),
             )
 
-        def round_x(s, g):
-            xb = stage.tile([P, SLICE, PACK], BF16, name="xb", bufs=2, align_bytes=64)
-            src = gathered[(s, g)][:].rearrange("p t n -> p n t")
-            if X_ROUND == "S":
-                nc.scalar.copy(out=xb[:], in_=src)
-            else:
-                nc.vector.tensor_copy(out=xb[:], in_=src)
-            rounded[(s, g)] = xb
+        def round_x(s):
+            xb = stage.tile([P, PASSES, SLICE, PACK], BF16, name="xb", bufs=2, align_bytes=64)
+            nc.vector.tensor_copy(out=xb[:], in_=gathered[s][:].rearrange("p g t n -> p g n t"))
+            rounded[s] = xb
 
-        def quantize_x(s, g):
-            cols = slice(s * SLICE, (s + 1) * SLICE)
+        def quantize_x(s):
             nc.vector.quantize_mx(
-                out=x_codes[:, g, cols].bitcast(FP8X4),
-                scales=x_scales[:, g, cols],
-                in_=rounded[(s, g)][:].rearrange("p n t -> p (n t)"),
+                out=x_codes[:, s, :, :].rearrange("p g n -> p (g n)").bitcast(FP8X4),
+                scales=x_scales[:, s, :, :].rearrange("p g n -> p (g n)"),
+                in_=rounded[s][:].rearrange("p g n t -> p (g n t)"),
             )
 
         def tile_info(i):
@@ -113,148 +100,148 @@ def tile_routed_moe_kernel(tc, xT, w1, w3, w2, gate, offs, pos1, pos2, out):
                 return ("w2", i - BIG_TILES, 0)
             return (("w1", "w3")[i % 2], i // 4, (i % 4) // 2)
 
+        def w2_group_of(e):
+            return [a for a, (e0, count) in enumerate(W2_GROUPS) if e0 <= e < e0 + count][0]
+
         w_codes = {}
         w_scales = {}
         grouped = {}
 
-        def split_copy(dst_s, src_s, dst_v, src_v, share, groups, v_cols_a_group):
-            if share > 0:
-                nc.scalar.copy(out=dst_s[:, 0:share], in_=src_s[:, 0:share])
-            if share < groups:
-                nc.vector.tensor_copy(out=dst_v[:, share * v_cols_a_group :], in_=src_v[:, share * v_cols_a_group :])
-
         def load_and_interleave(i):
             kind, e, g = tile_info(i)
-            raw = raws.tile([P, PACK * H], F32, name="raw")
-            grp = stage.tile([P, PACK * H], BF16, name="grp", align_bytes=64)
-            share = scalar_share(i)
+            raw = raws.tile([P, TILE], F32, name="raw")
             if kind == "w2":
-                e0, count = W2_GROUPS[e]
+                e0, count = W2_TILES[e]
+                a = w2_group_of(e0)
+                first = e0 - W2_GROUPS[a][0]
+                if first == 0:
+                    grouped[("w2", a)] = stage.tile([P, PASSES * TILE], BF16, name="grp", align_bytes=64)
+                width = count * PACK * N
                 nc.sync.dma_start(
-                    out=raw[:, 0 : count * PACK * N].rearrange("p (e r) -> p e r", e=count),
+                    out=raw[:, 0:width].rearrange("p (e r) -> p e r", e=count),
                     in_=w2[e0 : e0 + count].rearrange("e (p j) n -> p e (j n)", j=PACK),
                 )
-                for half in range(count):
-                    r = raw[:, half * PACK * N : (half + 1) * PACK * N]
-                    d = grp[:, half * PACK * N : (half + 1) * PACK * N]
-                    split_copy(
-                        d.rearrange("p (c j) -> p c j", j=PACK),
-                        r.rearrange("p (j c) -> p c j", j=PACK),
-                        d.rearrange("p (c j) -> p c j", j=PACK),
-                        r.rearrange("p (j c) -> p c j", j=PACK),
-                        share * N // 128,
-                        N,
-                        1,
-                    )
+                dst = grouped[("w2", a)][:, first * PACK * N : first * PACK * N + width].rearrange("p (e n j) -> p e n j", e=count, j=PACK)
+                src = raw[:, 0:width].rearrange("p (e j n) -> p e n j", e=count, j=PACK)
+                nc.scalar.copy(out=dst[:, :, 0:W2_SCALAR_COLS, :], in_=src[:, :, 0:W2_SCALAR_COLS, :])
+                nc.vector.tensor_copy(out=dst[:, :, W2_SCALAR_COLS:, :], in_=src[:, :, W2_SCALAR_COLS:, :])
             else:
-                src = w1 if kind == "w1" else w3
+                if g == 0:
+                    grouped[(kind, e)] = stage.tile([P, PASSES * TILE], BF16, name="grp", align_bytes=64)
+                w = w1 if kind == "w1" else w3
                 nc.sync.dma_start(
                     out=raw[:].rearrange("p (j c) -> p j c", j=PACK),
-                    in_=src[e, g * K_PASS : (g + 1) * K_PASS, :].rearrange("(p j) c -> p j c", j=PACK),
+                    in_=w[e, g * K_PASS : (g + 1) * K_PASS, :].rearrange("(p j) c -> p j c", j=PACK),
                 )
-                split_copy(
-                    grp[:].rearrange("p (c j) -> p c j", j=PACK),
-                    raw[:].rearrange("p (j c) -> p c j", j=PACK),
-                    grp[:].rearrange("p (c j) -> p c j", j=PACK),
-                    raw[:].rearrange("p (j c) -> p c j", j=PACK),
-                    share * H // 128,
-                    H,
-                    1,
-                )
-            grouped[i] = grp
+                dst = grouped[(kind, e)][:].rearrange("p (t g m j) -> p g m t j", t=4, g=PASSES, j=PACK)[:, g]
+                src = raw[:].rearrange("p (j m t) -> p m t j", j=PACK, t=4)
+                if i % 3 == 2:
+                    nc.vector.tensor_copy(out=dst, in_=src)
+                else:
+                    nc.scalar.copy(out=dst, in_=src)
 
-        def quantize_w(i):
-            kind, e, g = tile_info(i)
-            if g == 0:
-                passes = 1 if kind == "w2" else PASSES
-                w_codes[(kind, e)] = codes.tile([P, passes, H], U32, name=kind + "c", align_bytes=64)
-                w_scales[(kind, e)] = codes.tile([P, passes, H], U8, name=kind + "s", align_bytes=64)
-            width = W2_GROUPS[e][1] * N if kind == "w2" else H
+        def quantize_w(kind, e):
+            width = W2_GROUPS[e][1] * N if kind == "w2" else PASSES * H
+            w_codes[(kind, e)] = codes.tile([P, PASSES * H], U32, name=kind + "c", align_bytes=64)
+            w_scales[(kind, e)] = codes.tile([P, PASSES * H], U8, name=kind + "s", align_bytes=64)
             nc.vector.quantize_mx(
-                out=w_codes[(kind, e)][:, g, 0:width].bitcast(FP8X4),
-                scales=w_scales[(kind, e)][:, g, 0:width],
-                in_=grouped[i][:, 0 : PACK * width],
+                out=w_codes[(kind, e)][:, 0:width].bitcast(FP8X4),
+                scales=w_scales[(kind, e)][:, 0:width],
+                in_=grouped[(kind, e)][:, 0 : PACK * width],
             )
 
         banks = {}
         hidden = {}
 
         def layer1(e):
-            slots = slice(e * C, (e + 1) * C)
+            s = e // 2
+            slots = slice((e % 2) * C, (e % 2 + 1) * C)
             for kind in ("w1", "w3"):
-                bank = psum.tile([P, H], F32, name="bank_" + kind)
-                for g in range(PASSES):
-                    nc.tensor.matmul_mx(
-                        out=bank[:],
-                        lhsT=x_codes[:, g, slots].bitcast(FP8X4),
-                        lhsT_scale=x_scales[:, g, slots],
-                        rhs=w_codes[(kind, e)][:, g, :].bitcast(FP8X4),
-                        rhs_scale=w_scales[(kind, e)][:, g, :],
-                        start=(g == 0),
-                        stop=(g == PASSES - 1),
-                    )
+                bank = psum.tile([P, PACK, C], F32, name="bank_" + kind)
+                for t in range(PACK):
+                    for g in range(PASSES):
+                        cols = slice((t * PASSES + g) * P, (t * PASSES + g + 1) * P)
+                        nc.tensor.matmul_mx(
+                            out=bank[:, t, :],
+                            lhsT=w_codes[(kind, e)][:, cols].bitcast(FP8X4),
+                            lhsT_scale=w_scales[(kind, e)][:, cols],
+                            rhs=x_codes[:, s, g, slots].bitcast(FP8X4),
+                            rhs_scale=x_scales[:, s, g, slots],
+                            start=(g == 0),
+                            stop=(g == PASSES - 1),
+                        )
                 banks[(kind, e)] = bank
                 if kind == "w1":
-                    act = hid.tile([P, H], F32, name="act")
+                    act = hid.tile([P, PACK, C], F32, name="act")
                     nc.scalar.activation(out=act[:], in_=bank[:], func=GELU)
                     hidden[e] = act
 
         def gate_hidden(e):
-            h_rows = hid.tile([P, H], BF16, name="h_rows")
-            nc.vector.tensor_tensor(h_rows[:], hidden[e][:], banks[("w3", e)][:], MULT)
-            hidden[e] = h_rows
+            nc.vector.tensor_tensor(
+                h_bf[:, e, :, :],
+                hidden[e][:].rearrange("p t n -> p n t"),
+                banks[("w3", e)][:].rearrange("p t n -> p n t"),
+                MULT,
+            )
 
-        def turn_hidden(e):
-            words = hidden[e][:].bitcast(F32)
-            turned = psum.tile([P, 2, C], F32, name="turned")
-            for u in range(2):
-                nc.tensor.transpose(turned[:, u, :], words[:, u : H // 2 : 2], ident[:])
-            hb = hid.tile([P, C, PACK], BF16, name="hb", align_bytes=64)
-            nc.scalar.copy(out=hb[:].bitcast(F32), in_=turned[:].rearrange("p u n -> p n u"))
-            hidden[e] = hb
-
-        def quantize_hidden(e):
+        def quantize_hidden(a):
+            e0, count = W2_GROUPS[a]
             nc.vector.quantize_mx(
-                out=h_codes[:, e, :].bitcast(FP8X4),
-                scales=h_scales[:, e, :],
-                in_=hidden[e][:].rearrange("p n t -> p (n t)"),
+                out=h_codes[:, e0 : e0 + count, :].rearrange("p e n -> p (e n)").bitcast(FP8X4),
+                scales=h_scales[:, e0 : e0 + count, :].rearrange("p e n -> p (e n)"),
+                in_=h_bf[:, e0 : e0 + count, :, :].rearrange("p e n t -> p (e n t)"),
             )
 
         def layer2(a):
             e0, count = W2_GROUPS[a]
-            bank = psum.tile([P, NB, 2, C], F32, name="bank_y")
             for nb in range(NB):
-                for half in range(count):
-                    cols = slice(half * N + nb * P, half * N + (nb + 1) * P)
+                bank = psum.tile([P, PACK, C], F32, name="bank_y", bufs=3)
+                for k in range(count):
+                    cols = slice(k * N + nb * P, k * N + (nb + 1) * P)
                     nc.tensor.matmul_mx(
-                        out=bank[:, nb, half, :],
-                        lhsT=w_codes[("w2", a)][:, 0, cols].bitcast(FP8X4),
-                        lhsT_scale=w_scales[("w2", a)][:, 0, cols],
-                        rhs=h_codes[:, e0 + half, :].bitcast(FP8X4),
-                        rhs_scale=h_scales[:, e0 + half, :],
+                        out=bank[:, k, :],
+                        lhsT=w_codes[("w2", a)][:, cols].bitcast(FP8X4),
+                        lhsT_scale=w_scales[("w2", a)][:, cols],
+                        rhs=h_codes[:, e0 + k, :].bitcast(FP8X4),
+                        rhs_scale=h_scales[:, e0 + k, :],
                         start=True,
                         stop=True,
                     )
                 nc.scalar.copy(
                     out=y_tiles[nb][:, e0 * C : (e0 + count) * C],
-                    in_=bank[:, nb, 0:count, :].rearrange("p h c -> p (h c)"),
+                    in_=bank[:, 0:count, :].rearrange("p k c -> p (k c)"),
                 )
 
         for g in range(PASSES):
             for t in range(PACK):
                 gather(0, g, t)
-        round_x(0, 0)
-        round_x(0, 1)
-        quantize_x(0, 0)
-        quantize_x(0, 1)
+        round_x(0)
+        quantize_x(0)
 
         later = {}
 
         def defer(step, fn, arg):
             later.setdefault(step, []).append((fn, arg))
 
+        def unit_done(i, step):
+            kind, e, g = tile_info(i)
+            if kind == "w2":
+                e0, count = W2_TILES[e]
+                a = w2_group_of(e0)
+                if e0 + count == W2_GROUPS[a][0] + W2_GROUPS[a][1]:
+                    quantize_w("w2", a)
+                    defer(step, layer2, a)
+            elif g == PASSES - 1:
+                quantize_w(kind, e)
+                if kind == "w3":
+                    defer(step, layer1, e)
+                    defer(step + 1, gate_hidden, e)
+                    a = w2_group_of(e)
+                    if e == W2_GROUPS[a][0] + W2_GROUPS[a][1] - 1:
+                        defer(step + 2, quantize_hidden, a)
+
         done = 0
-        for i in range(N_TILES + 6):
+        for i in range(N_TILES + 4):
             if i < N_TILES:
                 load_and_interleave(i)
                 if i == 5:
@@ -262,27 +249,15 @@ def tile_routed_moe_kernel(tc, xT, w1, w3, w2, gate, offs, pos1, pos2, out):
                     nc.sync.dma_start(pos2_t[:], pos2)
                 s = i // 8 + 1
                 k = i % 8
+                if 2 <= s <= SLICES and k == 0:
+                    round_x(s - 1)
+                if 2 <= s <= SLICES and k == 1:
+                    quantize_x(s - 1)
                 if s < SLICES:
                     gather(s, k // PACK, k % PACK)
-                    if k == 5:
-                        round_x(s, 0)
-                    if k == 6:
-                        quantize_x(s, 0)
-                if 2 <= s <= SLICES and k == 0:
-                    round_x(s - 1, 1)
-                if 2 <= s <= SLICES and k == 1:
-                    quantize_x(s - 1, 1)
             lag = min(LAG, max(0, N_TILES - 1 - i))
             while done < N_TILES and done <= i - lag:
-                quantize_w(done)
-                kind, e, g = tile_info(done)
-                if kind == "w3" and g == 1:
-                    defer(i, layer1, e)
-                    defer(i + 1, gate_hidden, e)
-                    defer(i + 1, turn_hidden, e)
-                    defer(i + 2, quantize_hidden, e)
-                if kind == "w2":
-                    defer(i, layer2, e)
+                unit_done(done, i)
                 done += 1
             for fn, arg in later.get(i, []):
                 fn(arg)
@@ -292,8 +267,8 @@ def tile_routed_moe_kernel(tc, xT, w1, w3, w2, gate, offs, pos1, pos2, out):
                 nc.sync.dma_start(gate_tiles[r][nb][:], gate[r, nb * P : (nb + 1) * P, :])
 
         for nb in range(NB):
-            first = hid.tile([P, T], F32, name="first")
-            second = hid.tile([P, T], F32, name="second")
+            first = hid.tile([P, T], F32, name="first", bufs=1)
+            second = hid.tile([P, T], F32, name="second", bufs=1)
             nc.vector.tensor_tensor(first[:], y_tiles[nb][:].indirect(pos1_t[:]), gate_tiles[0][nb][:], MULT)
             nc.vector.tensor_tensor(second[:], y_tiles[nb][:].indirect(pos2_t[:]), gate_tiles[1][nb][:], MULT)
             total = hid.tile([P, T], F32, name="total")

@@ -12,6 +12,7 @@ U16 = mybir.dt.uint16
 U8 = mybir.dt.uint8
 FP8X4 = mybir.dt.float8_e4m3fn_x4
 GELU = mybir.ActivationFunctionType.Gelu_apprx_tanh
+COPY = mybir.ActivationFunctionType.Copy
 MULT = mybir.AluOpType.mult
 ADD = mybir.AluOpType.add
 
@@ -19,8 +20,6 @@ P = 128
 PACK = 4
 K_PASS = P * PACK
 PASSES = K // K_PASS
-SLICE = 256
-SLICES = E * C // SLICE
 NB = N // P
 TILE = PACK * H
 RAW_BUFS = 10
@@ -54,18 +53,19 @@ def tile_routed_moe_kernel(tc, xT, w1, w3, w2, gate, offs, pos1, pos2, out):
         nc.vector.memset(warm[:], 0.0)
         nc.scalar.activation(out=warm_out[:], in_=warm[:], func=GELU)
 
-        x_view = xT.rearrange("(g p t) n -> g p t n", p=P, t=PACK)
-        planes = []
+        x_bf = []
         for g in range(PASSES):
-            row = []
-            for t in range(PACK):
-                plane = keep.tile([P, T], F32, name="plane%d%d" % (g, t))
-                nc.sync.dma_start(plane[:], x_view[g, :, t, :])
-                row.append(plane)
-            planes.append(row)
+            x_raw = raws.tile([P, TILE], F32, name="raw")
+            nc.sync.dma_start(
+                out=x_raw[:].rearrange("p (t n) -> p t n", t=PACK),
+                in_=xT[g * K_PASS : (g + 1) * K_PASS, :].rearrange("(p t) n -> p t n", t=PACK),
+            )
+            planes = keep.tile([P, PACK, T], BF16, name="x_bf%d" % g)
+            nc.vector.tensor_copy(out=planes[:].rearrange("p t n -> p (t n)"), in_=x_raw[:])
+            x_bf.append(planes)
 
-        x_codes = keep.tile([P, SLICES, PASSES, SLICE], U32, name="x_codes", align_bytes=64)
-        x_scales = keep.tile([P, SLICES, PASSES, SLICE], U8, name="x_scales", align_bytes=64)
+        x_codes = keep.tile([P, E, PASSES, C], U32, name="x_codes", align_bytes=64)
+        x_scales = keep.tile([P, E, PASSES, C], U8, name="x_scales", align_bytes=64)
         h_codes = keep.tile([P, E, C], U32, name="h_codes", align_bytes=64)
         h_scales = keep.tile([P, E, C], U8, name="h_scales", align_bytes=64)
         h_bf = keep.tile([P, E, C, PACK], BF16, name="h_bf", align_bytes=64)
@@ -73,26 +73,21 @@ def tile_routed_moe_kernel(tc, xT, w1, w3, w2, gate, offs, pos1, pos2, out):
         gate_tiles = [[keep.tile([P, T], F32, name="gate%d%d" % (r, nb)) for nb in range(NB)] for r in range(2)]
 
         gathered = {}
-        rounded = {}
 
-        def gather(s, g, t):
+        def gather(e, g, t):
             if g == 0 and t == 0:
-                gathered[s] = stage.tile([P, PASSES, PACK, SLICE], F32, name="g4", bufs=1)
-            nc.vector.tensor_copy(
-                gathered[s][:, g, t, :],
-                planes[g][t][:].indirect(offs_t[:, s * SLICE // 16 : (s + 1) * SLICE // 16]),
+                gathered[e] = stage.tile([P, PASSES, C, PACK], BF16, name="xb", bufs=2, align_bytes=64)
+            nc.scalar.activation(
+                out=gathered[e][:, g, :, t],
+                in_=x_bf[g][:, t, :].indirect(offs_t[:, e * C // 16 : (e + 1) * C // 16]),
+                func=COPY,
             )
 
-        def round_x(s):
-            xb = stage.tile([P, PASSES, SLICE, PACK], BF16, name="xb", bufs=2, align_bytes=64)
-            nc.vector.tensor_copy(out=xb[:], in_=gathered[s][:].rearrange("p g t n -> p g n t"))
-            rounded[s] = xb
-
-        def quantize_x(s):
+        def quantize_x(e):
             nc.vector.quantize_mx(
-                out=x_codes[:, s, :, :].rearrange("p g n -> p (g n)").bitcast(FP8X4),
-                scales=x_scales[:, s, :, :].rearrange("p g n -> p (g n)"),
-                in_=rounded[s][:].rearrange("p g n t -> p (g n t)"),
+                out=x_codes[:, e, :, :].rearrange("p g n -> p (g n)").bitcast(FP8X4),
+                scales=x_scales[:, e, :, :].rearrange("p g n -> p (g n)"),
+                in_=gathered[e][:].rearrange("p g n t -> p (g n t)"),
             )
 
         def tile_info(i):
@@ -135,10 +130,10 @@ def tile_routed_moe_kernel(tc, xT, w1, w3, w2, gate, offs, pos1, pos2, out):
                 )
                 dst = grouped[(kind, e)][:].rearrange("p (t g m j) -> p g m t j", t=4, g=PASSES, j=PACK)[:, g]
                 src = raw[:].rearrange("p (j m t) -> p m t j", j=PACK, t=4)
-                if i % 3 == 2:
-                    nc.vector.tensor_copy(out=dst, in_=src)
-                else:
+                if i % 4 == 1:
                     nc.scalar.copy(out=dst, in_=src)
+                else:
+                    nc.vector.tensor_copy(out=dst, in_=src)
 
         def quantize_w(kind, e):
             width = W2_GROUPS[e][1] * N if kind == "w2" else PASSES * H
@@ -154,8 +149,6 @@ def tile_routed_moe_kernel(tc, xT, w1, w3, w2, gate, offs, pos1, pos2, out):
         hidden = {}
 
         def layer1(e):
-            s = e // 2
-            slots = slice((e % 2) * C, (e % 2 + 1) * C)
             for kind in ("w1", "w3"):
                 bank = psum.tile([P, PACK, C], F32, name="bank_" + kind)
                 for t in range(PACK):
@@ -165,8 +158,8 @@ def tile_routed_moe_kernel(tc, xT, w1, w3, w2, gate, offs, pos1, pos2, out):
                             out=bank[:, t, :],
                             lhsT=w_codes[(kind, e)][:, cols].bitcast(FP8X4),
                             lhsT_scale=w_scales[(kind, e)][:, cols],
-                            rhs=x_codes[:, s, g, slots].bitcast(FP8X4),
-                            rhs_scale=x_scales[:, s, g, slots],
+                            rhs=x_codes[:, e, g, :].bitcast(FP8X4),
+                            rhs_scale=x_scales[:, e, g, :],
                             start=(g == 0),
                             stop=(g == PASSES - 1),
                         )
@@ -215,7 +208,6 @@ def tile_routed_moe_kernel(tc, xT, w1, w3, w2, gate, offs, pos1, pos2, out):
         for g in range(PASSES):
             for t in range(PACK):
                 gather(0, g, t)
-        round_x(0)
         quantize_x(0)
 
         later = {}
@@ -247,14 +239,13 @@ def tile_routed_moe_kernel(tc, xT, w1, w3, w2, gate, offs, pos1, pos2, out):
                 if i == 5:
                     nc.sync.dma_start(pos1_t[:], pos1)
                     nc.sync.dma_start(pos2_t[:], pos2)
-                s = i // 8 + 1
-                k = i % 8
-                if 2 <= s <= SLICES and k == 0:
-                    round_x(s - 1)
-                if 2 <= s <= SLICES and k == 1:
-                    quantize_x(s - 1)
-                if s < SLICES:
-                    gather(s, k // PACK, k % PACK)
+                nxt = i // 4 + 1
+                k = i % 4
+                if 2 <= nxt <= E and k == 0:
+                    quantize_x(nxt - 1)
+                if nxt < E:
+                    gather(nxt, k // 2, 2 * (k % 2))
+                    gather(nxt, k // 2, 2 * (k % 2) + 1)
             lag = min(LAG, max(0, N_TILES - 1 - i))
             while done < N_TILES and done <= i - lag:
                 unit_done(done, i)

@@ -29,7 +29,8 @@ BIG_TILES = 4 * E
 W2_GROUPS = [(0, 4), (4, 2), (6, 1), (7, 1)]
 W2_TILES = [(0, 2), (2, 2), (4, 2), (6, 1), (7, 1)]
 N_TILES = BIG_TILES + len(W2_TILES)
-W2_SCALAR_COLS = 88
+W2_SCALAR_COLS = 160
+LAST_GATHER_TILE = 4 * (E - 1)
 
 
 def tile_routed_moe_kernel(tc, xT, w1, w3, w2, gate, offs, pos1, pos2, out):
@@ -130,7 +131,7 @@ def tile_routed_moe_kernel(tc, xT, w1, w3, w2, gate, offs, pos1, pos2, out):
                 )
                 dst = grouped[(kind, e)][:].rearrange("p (t g m j) -> p g m t j", t=4, g=PASSES, j=PACK)[:, g]
                 src = raw[:].rearrange("p (j m t) -> p m t j", j=PACK, t=4)
-                if i % 4 == 1:
+                if i % 4 == 1 or (i >= LAST_GATHER_TILE and i % 4 == 3):
                     nc.scalar.copy(out=dst, in_=src)
                 else:
                     nc.vector.tensor_copy(out=dst, in_=src)

@@ -39,6 +39,7 @@ def tile_routed_moe_kernel(tc, xT, w1, w3, w2, gate, offs, pos1, pos2, out):
         lists = ctx.enter_context(tc.tile_pool(name="lists", bufs=1))
         keep = ctx.enter_context(tc.tile_pool(name="keep", bufs=1))
         raws = ctx.enter_context(tc.tile_pool(name="raws", bufs=RAW_BUFS))
+        raws_s = ctx.enter_context(tc.tile_pool(name="raws_s", bufs=2))
         stage = ctx.enter_context(tc.tile_pool(name="stage", bufs=GRP_BUFS))
         codes = ctx.enter_context(tc.tile_pool(name="codes", bufs=2))
         hid = ctx.enter_context(tc.tile_pool(name="hid", bufs=2))
@@ -105,7 +106,11 @@ def tile_routed_moe_kernel(tc, xT, w1, w3, w2, gate, offs, pos1, pos2, out):
 
         def load_and_interleave(i):
             kind, e, g = tile_info(i)
-            raw = raws.tile([P, TILE], F32, name="raw")
+            on_scalar = kind != "w2" and (i % 4 == 1 or (i >= LAST_GATHER_TILE and i % 4 == 3))
+            if on_scalar:
+                raw = raws_s.tile([P, TILE], F32, name="raw_s")
+            else:
+                raw = raws.tile([P, TILE], F32, name="raw")
             if kind == "w2":
                 e0, count = W2_TILES[e]
                 a = w2_group_of(e0)
@@ -125,13 +130,14 @@ def tile_routed_moe_kernel(tc, xT, w1, w3, w2, gate, offs, pos1, pos2, out):
                 if g == 0:
                     grouped[(kind, e)] = stage.tile([P, PASSES * TILE], BF16, name="grp", align_bytes=64)
                 w = w1 if kind == "w1" else w3
-                nc.sync.dma_start(
+                queue = nc.scalar if (on_scalar and i >= 8) else nc.sync
+                queue.dma_start(
                     out=raw[:].rearrange("p (j c) -> p j c", j=PACK),
                     in_=w[e, g * K_PASS : (g + 1) * K_PASS, :].rearrange("(p j) c -> p j c", j=PACK),
                 )
                 dst = grouped[(kind, e)][:].rearrange("p (t g m j) -> p g m t j", t=4, g=PASSES, j=PACK)[:, g]
                 src = raw[:].rearrange("p (j m t) -> p m t j", j=PACK, t=4)
-                if i % 4 == 1 or (i >= LAST_GATHER_TILE and i % 4 == 3):
+                if on_scalar:
                     nc.scalar.copy(out=dst, in_=src)
                 else:
                     nc.vector.tensor_copy(out=dst, in_=src)

@@ -135,8 +135,8 @@ def tile_routed_moe_kernel(tc, xT, w1, w3, w2, gate, offs, pos1, pos2, out):
                     out=raw[:].rearrange("p (j c) -> p j c", j=PACK),
                     in_=w[e, g * K_PASS : (g + 1) * K_PASS, :].rearrange("(p j) c -> p j c", j=PACK),
                 )
-                dst = grouped[(kind, e)][:].rearrange("p (t g m j) -> p g m t j", t=4, g=PASSES, j=PACK)[:, g]
-                src = raw[:].rearrange("p (j m t) -> p m t j", j=PACK, t=4)
+                dst = grouped[(kind, e)][:].rearrange("p (t g m j) -> p g m j t", t=4, g=PASSES, j=PACK)[:, g]
+                src = raw[:].rearrange("p (j m t) -> p m j t", j=PACK, t=4)
                 if on_scalar:
                     nc.scalar.copy(out=dst, in_=src)
                 else:

@@ -22,7 +22,7 @@ K_PASS = P * PACK
 PASSES = K // K_PASS
 NB = N // P
 TILE = PACK * H
-RAW_BUFS = 10
+RAW_BUFS = 7
 GRP_BUFS = 4
 LAG = 2
 BIG_TILES = 4 * E
@@ -40,6 +40,7 @@ def tile_routed_moe_kernel(tc, xT, w1, w3, w2, gate, offs, pos1, pos2, out):
         keep = ctx.enter_context(tc.tile_pool(name="keep", bufs=1))
         raws = ctx.enter_context(tc.tile_pool(name="raws", bufs=RAW_BUFS))
         raws_s = ctx.enter_context(tc.tile_pool(name="raws_s", bufs=2))
+        raws_v = ctx.enter_context(tc.tile_pool(name="raws_v", bufs=3))
         stage = ctx.enter_context(tc.tile_pool(name="stage", bufs=GRP_BUFS))
         codes = ctx.enter_context(tc.tile_pool(name="codes", bufs=2))
         hid = ctx.enter_context(tc.tile_pool(name="hid", bufs=2))
@@ -109,6 +110,8 @@ def tile_routed_moe_kernel(tc, xT, w1, w3, w2, gate, offs, pos1, pos2, out):
             on_scalar = kind != "w2" and (i % 4 == 1 or (i >= LAST_GATHER_TILE and i % 4 == 3))
             if on_scalar:
                 raw = raws_s.tile([P, TILE], F32, name="raw_s")
+            elif kind == "w3":
+                raw = raws_v.tile([P, TILE], F32, name="raw_v")
             else:
                 raw = raws.tile([P, TILE], F32, name="raw")
             if kind == "w2":
@@ -130,7 +133,7 @@ def tile_routed_moe_kernel(tc, xT, w1, w3, w2, gate, offs, pos1, pos2, out):
                 if g == 0:
                     grouped[(kind, e)] = stage.tile([P, PASSES * TILE], BF16, name="grp", align_bytes=64)
                 w = w1 if kind == "w1" else w3
-                queue = nc.scalar if (on_scalar and i >= 8) else nc.sync
+                queue = nc.scalar if ((on_scalar and i >= 8) or (kind == "w3" and i >= 12)) else nc.sync
                 queue.dma_start(
                     out=raw[:].rearrange("p (j c) -> p j c", j=PACK),
                     in_=w[e, g * K_PASS : (g + 1) * K_PASS, :].rearrange("(p j) c -> p j c", j=PACK),

@@ -25,6 +25,7 @@ TILE = PACK * H
 RAW_BUFS = 7
 GRP_BUFS = 4
 LAG = 2
+AHEAD = 7
 BIG_TILES = 4 * E
 W2_GROUPS = [(0, 4), (4, 2), (6, 1), (7, 1)]
 W2_TILES = [(0, 2), (2, 2), (4, 2), (6, 1), (7, 1)]
@@ -105,10 +106,38 @@ def tile_routed_moe_kernel(tc, xT, w1, w3, w2, gate, offs, pos1, pos2, out):
         w_scales = {}
         grouped = {}
 
+        raw_of = {}
+
+        def scalar_interleaves(i):
+            return i < BIG_TILES and (i % 4 == 1 or (i >= LAST_GATHER_TILE and i % 4 == 3))
+
+        def on_scalar_queue(i):
+            return (scalar_interleaves(i) and i >= 8) or (i < BIG_TILES and i % 2 == 1 and i >= 12)
+
+        def load_big(i):
+            kind, e, g = tile_info(i)
+            if scalar_interleaves(i):
+                raw = raws_s.tile([P, TILE], F32, name="raw_s")
+            elif kind == "w3":
+                raw = raws_v.tile([P, TILE], F32, name="raw_v")
+            else:
+                raw = raws.tile([P, TILE], F32, name="raw")
+            w = w1 if kind == "w1" else w3
+            queue = nc.scalar if on_scalar_queue(i) else nc.sync
+            queue.dma_start(
+                out=raw[:].rearrange("p (j c) -> p j c", j=PACK),
+                in_=w[e, g * K_PASS : (g + 1) * K_PASS, :].rearrange("(p j) c -> p j c", j=PACK),
+            )
+            raw_of[i] = raw
+
         def load_and_interleave(i):
             kind, e, g = tile_info(i)
-            on_scalar = kind != "w2" and (i % 4 == 1 or (i >= LAST_GATHER_TILE and i % 4 == 3))
-            if on_scalar:
+            on_scalar = scalar_interleaves(i)
+            if kind != "w2":
+                if i not in raw_of:
+                    load_big(i)
+                raw = raw_of[i]
+            elif on_scalar:
                 raw = raws_s.tile([P, TILE], F32, name="raw_s")
             elif kind == "w3":
                 raw = raws_v.tile([P, TILE], F32, name="raw_v")
@@ -132,12 +161,6 @@ def tile_routed_moe_kernel(tc, xT, w1, w3, w2, gate, offs, pos1, pos2, out):
             else:
                 if g == 0:
                     grouped[(kind, e)] = stage.tile([P, PASSES * TILE], BF16, name="grp", align_bytes=64)
-                w = w1 if kind == "w1" else w3
-                queue = nc.scalar if ((on_scalar and i >= 8) or (kind == "w3" and i >= 12)) else nc.sync
-                queue.dma_start(
-                    out=raw[:].rearrange("p (j c) -> p j c", j=PACK),
-                    in_=w[e, g * K_PASS : (g + 1) * K_PASS, :].rearrange("(p j) c -> p j c", j=PACK),
-                )
                 dst = grouped[(kind, e)][:].rearrange("p (t g m j) -> p g m j t", t=4, g=PASSES, j=PACK)[:, g]
                 src = raw[:].rearrange("p (j m t) -> p m j t", j=PACK, t=4)
                 if on_scalar:
@@ -242,10 +265,21 @@ def tile_routed_moe_kernel(tc, xT, w1, w3, w2, gate, offs, pos1, pos2, out):
                     if e == W2_GROUPS[a][0] + W2_GROUPS[a][1] - 1:
                         defer(step + 2, quantize_hidden, a)
 
+        ask_at = {}
+        for ring_depth, tenants in ((2, [i for i in range(BIG_TILES) if scalar_interleaves(i)]),
+                                    (3, [i for i in range(BIG_TILES) if i % 2 == 1 and not scalar_interleaves(i)])):
+            step = 0
+            for k, i in enumerate(tenants):
+                step = max(step, i - AHEAD, tenants[k - ring_depth] + 1) if on_scalar_queue(i) else i
+                if on_scalar_queue(i):
+                    ask_at.setdefault(step, []).append(i)
+
         done = 0
         for i in range(N_TILES + 4):
             if i < N_TILES:
                 load_and_interleave(i)
+                for ahead in ask_at.get(i, []):
+                    load_big(ahead)
                 if i == 5:
                     nc.sync.dma_start(pos1_t[:], pos1)
                     nc.sync.dma_start(pos2_t[:], pos2)

@@ -31,6 +31,7 @@ W2_GROUPS = [(0, 4), (4, 2), (6, 1), (7, 1)]
 W2_TILES = [(0, 2), (2, 2), (4, 2), (6, 1), (7, 1)]
 N_TILES = BIG_TILES + len(W2_TILES)
 W2_SCALAR_COLS = 160
+W2_SCALAR_COLS_LAST = 88
 LAST_GATHER_TILE = 4 * (E - 1)
 
 
@@ -74,7 +75,7 @@ def tile_routed_moe_kernel(tc, xT, w1, w3, w2, gate, offs, pos1, pos2, out):
         h_scales = keep.tile([P, E, C], U8, name="h_scales", align_bytes=64)
         h_bf = keep.tile([P, E, C, PACK], BF16, name="h_bf", align_bytes=64)
         y_tiles = [keep.tile([P, E * C], F32, name="y%d" % nb) for nb in range(NB)]
-        gate_tiles = [[keep.tile([P, T], F32, name="gate%d%d" % (r, nb)) for nb in range(NB)] for r in range(2)]
+        gate_tiles = [keep.tile([P, 2, T], F32, name="gate%d" % nb) for nb in range(NB)]
 
         gathered = {}
 
@@ -156,8 +157,9 @@ def tile_routed_moe_kernel(tc, xT, w1, w3, w2, gate, offs, pos1, pos2, out):
                 )
                 dst = grouped[("w2", a)][:, first * PACK * N : first * PACK * N + width].rearrange("p (e n j) -> p e n j", e=count, j=PACK)
                 src = raw[:, 0:width].rearrange("p (e j n) -> p e n j", e=count, j=PACK)
-                nc.scalar.copy(out=dst[:, :, 0:W2_SCALAR_COLS, :], in_=src[:, :, 0:W2_SCALAR_COLS, :])
-                nc.vector.tensor_copy(out=dst[:, :, W2_SCALAR_COLS:, :], in_=src[:, :, W2_SCALAR_COLS:, :])
+                share = W2_SCALAR_COLS if count > 1 else W2_SCALAR_COLS_LAST
+                nc.scalar.copy(out=dst[:, :, 0:share, :], in_=src[:, :, 0:share, :])
+                nc.vector.tensor_copy(out=dst[:, :, share:, :], in_=src[:, :, share:, :])
             else:
                 if g == 0:
                     grouped[(kind, e)] = stage.tile([P, PASSES * TILE], BF16, name="grp", align_bytes=64)
@@ -298,14 +300,24 @@ def tile_routed_moe_kernel(tc, xT, w1, w3, w2, gate, offs, pos1, pos2, out):
                 fn(arg)
 
         for nb in range(NB):
-            for r in range(2):
-                nc.sync.dma_start(gate_tiles[r][nb][:], gate[r, nb * P : (nb + 1) * P, :])
+            nc.sync.dma_start(gate_tiles[nb][:], gate[:, nb * P : (nb + 1) * P, :].rearrange("r p t -> p r t"))
 
-        for nb in range(NB):
-            first = hid.tile([P, T], F32, name="first", bufs=1)
-            second = hid.tile([P, T], F32, name="second", bufs=1)
-            nc.vector.tensor_tensor(first[:], y_tiles[nb][:].indirect(pos1_t[:]), gate_tiles[0][nb][:], MULT)
-            nc.vector.tensor_tensor(second[:], y_tiles[nb][:].indirect(pos2_t[:]), gate_tiles[1][nb][:], MULT)
+        weighted = {}
+
+        def fetch(nb, r):
+            weighted[(nb, r)] = hid.tile([P, T], F32, name="weighted%d" % r, bufs=2)
+            nc.vector.tensor_tensor(
+                weighted[(nb, r)][:], y_tiles[nb][:].indirect((pos1_t, pos2_t)[r][:]), gate_tiles[nb][:, r, :], MULT
+            )
+
+        def add_and_store(nb):
             total = hid.tile([P, T], F32, name="total")
-            nc.vector.tensor_tensor(total[:], first[:], second[:], ADD)
+            nc.vector.tensor_tensor(total[:], weighted[(nb, 0)][:], weighted[(nb, 1)][:], ADD)
             nc.sync.dma_start(out[nb * P : (nb + 1) * P, :], total[:])
+
+        fetch(0, 0)
+        fetch(0, 1)
+        fetch(1, 0)
+        add_and_store(0)
+        fetch(1, 1)
+        add_and_store(1)

@@ -25,13 +25,12 @@ TILE = PACK * H
 RAW_BUFS = 7
 GRP_BUFS = 4
 LAG = 2
-AHEAD = 7
+AHEAD = 11
 BIG_TILES = 4 * E
 W2_GROUPS = [(0, 4), (4, 2), (6, 1), (7, 1)]
 W2_TILES = [(0, 2), (2, 2), (4, 2), (6, 1), (7, 1)]
 N_TILES = BIG_TILES + len(W2_TILES)
-W2_SCALAR_COLS = 160
-W2_SCALAR_COLS_LAST = 88
+W2_SCALAR_COLS = 88
 LAST_GATHER_TILE = 4 * (E - 1)
 
 
@@ -41,7 +40,7 @@ def tile_routed_moe_kernel(tc, xT, w1, w3, w2, gate, offs, pos1, pos2, out):
         lists = ctx.enter_context(tc.tile_pool(name="lists", bufs=1))
         keep = ctx.enter_context(tc.tile_pool(name="keep", bufs=1))
         raws = ctx.enter_context(tc.tile_pool(name="raws", bufs=RAW_BUFS))
-        raws_s = ctx.enter_context(tc.tile_pool(name="raws_s", bufs=2))
+        raws_s = ctx.enter_context(tc.tile_pool(name="raws_s", bufs=3))
         raws_v = ctx.enter_context(tc.tile_pool(name="raws_v", bufs=3))
         stage = ctx.enter_context(tc.tile_pool(name="stage", bufs=GRP_BUFS))
         codes = ctx.enter_context(tc.tile_pool(name="codes", bufs=2))
@@ -113,7 +112,7 @@ def tile_routed_moe_kernel(tc, xT, w1, w3, w2, gate, offs, pos1, pos2, out):
             return i < BIG_TILES and (i % 4 == 1 or (i >= LAST_GATHER_TILE and i % 4 == 3))
 
         def on_scalar_queue(i):
-            return (scalar_interleaves(i) and i >= 8) or (i < BIG_TILES and i % 2 == 1 and i >= 12)
+            return i < BIG_TILES and i % 2 == 1 and i >= 12
 
         def load_big(i):
             kind, e, g = tile_info(i)
@@ -157,7 +156,7 @@ def tile_routed_moe_kernel(tc, xT, w1, w3, w2, gate, offs, pos1, pos2, out):
                 )
                 dst = grouped[("w2", a)][:, first * PACK * N : first * PACK * N + width].rearrange("p (e n j) -> p e n j", e=count, j=PACK)
                 src = raw[:, 0:width].rearrange("p (e j n) -> p e n j", e=count, j=PACK)
-                share = W2_SCALAR_COLS if count > 1 else W2_SCALAR_COLS_LAST
+                share = W2_SCALAR_COLS
                 nc.scalar.copy(out=dst[:, :, 0:share, :], in_=src[:, :, 0:share, :])
                 nc.vector.tensor_copy(out=dst[:, :, share:, :], in_=src[:, :, share:, :])
             else:
@@ -268,7 +267,7 @@ def tile_routed_moe_kernel(tc, xT, w1, w3, w2, gate, offs, pos1, pos2, out):
                         defer(step + 2, quantize_hidden, a)
 
         ask_at = {}
-        for ring_depth, tenants in ((2, [i for i in range(BIG_TILES) if scalar_interleaves(i)]),
+        for ring_depth, tenants in ((3, [i for i in range(BIG_TILES) if scalar_interleaves(i)]),
                                     (3, [i for i in range(BIG_TILES) if i % 2 == 1 and not scalar_interleaves(i)])):
             step = 0
             for k, i in enumerate(tenants):

@@ -29,7 +29,22 @@ AHEAD = 11
 BIG_TILES = 4 * E
 W2_GROUPS = [(0, 4), (4, 2), (6, 1), (7, 1)]
 W2_TILES = [(0, 2), (2, 2), (4, 2), (6, 1), (7, 1)]
+W2_AFTER = [31, 31, 31, 31, 31]
 N_TILES = BIG_TILES + len(W2_TILES)
+END_FROM = BIG_TILES
+
+
+def load_order():
+    order = []
+    for big in range(BIG_TILES):
+        order.append((("w1", "w3")[big % 2], big // 4, (big % 4) // 2, big))
+        for k2, after in enumerate(W2_AFTER):
+            if after == big:
+                order.append(("w2", k2, 0, -1))
+    return order
+
+
+STREAM = load_order()
 W2_SCALAR_COLS = 88
 LAST_GATHER_TILE = 4 * (E - 1)
 
@@ -95,9 +110,10 @@ def tile_routed_moe_kernel(tc, xT, w1, w3, w2, gate, offs, pos1, pos2, out):
             )
 
         def tile_info(i):
-            if i >= BIG_TILES:
-                return ("w2", i - BIG_TILES, 0)
-            return (("w1", "w3")[i % 2], i // 4, (i % 4) // 2)
+            return STREAM[i][0:3]
+
+        def big_of(i):
+            return STREAM[i][3]
 
         def w2_group_of(e):
             return [a for a, (e0, count) in enumerate(W2_GROUPS) if e0 <= e < e0 + count][0]
@@ -109,10 +125,12 @@ def tile_routed_moe_kernel(tc, xT, w1, w3, w2, gate, offs, pos1, pos2, out):
         raw_of = {}
 
         def scalar_interleaves(i):
-            return i < BIG_TILES and (i % 4 == 1 or (i >= LAST_GATHER_TILE and i % 4 == 3))
+            b = big_of(i)
+            return b >= 0 and (b % 4 == 1 or (b >= LAST_GATHER_TILE and b % 4 == 3))
 
         def on_scalar_queue(i):
-            return i < BIG_TILES and i % 2 == 1 and i >= 12
+            b = big_of(i)
+            return b >= 0 and b % 2 == 1 and b >= 12
 
         def load_big(i):
             kind, e, g = tile_info(i)
@@ -239,6 +257,13 @@ def tile_routed_moe_kernel(tc, xT, w1, w3, w2, gate, offs, pos1, pos2, out):
                     in_=bank[:, 0:count, :].rearrange("p k c -> p (k c)"),
                 )
 
+        halves_ready = {}
+
+        def second_layer_if_ready(a):
+            halves_ready[a] = halves_ready.get(a, 0) + 1
+            if halves_ready[a] == 2:
+                layer2(a)
+
         for g in range(PASSES):
             for t in range(PACK):
                 gather(0, g, t)
@@ -256,7 +281,7 @@ def tile_routed_moe_kernel(tc, xT, w1, w3, w2, gate, offs, pos1, pos2, out):
                 a = w2_group_of(e0)
                 if e0 + count == W2_GROUPS[a][0] + W2_GROUPS[a][1]:
                     quantize_w("w2", a)
-                    defer(step, layer2, a)
+                    defer(step, second_layer_if_ready, a)
             elif g == PASSES - 1:
                 quantize_w(kind, e)
                 if kind == "w3":
@@ -265,15 +290,21 @@ def tile_routed_moe_kernel(tc, xT, w1, w3, w2, gate, offs, pos1, pos2, out):
                     a = w2_group_of(e)
                     if e == W2_GROUPS[a][0] + W2_GROUPS[a][1] - 1:
                         defer(step + 2, quantize_hidden, a)
+                        defer(step + 2, second_layer_if_ready, a)
 
         ask_at = {}
-        for ring_depth, tenants in ((3, [i for i in range(BIG_TILES) if scalar_interleaves(i)]),
-                                    (3, [i for i in range(BIG_TILES) if i % 2 == 1 and not scalar_interleaves(i)])):
+        for ring_depth, tenants in ((3, [i for i in range(N_TILES) if scalar_interleaves(i)]),
+                                    (3, [i for i in range(N_TILES) if big_of(i) % 2 == 1 and big_of(i) >= 0 and not scalar_interleaves(i)])):
             step = 0
             for k, i in enumerate(tenants):
                 step = max(step, i - AHEAD, tenants[k - ring_depth] + 1) if on_scalar_queue(i) else i
                 if on_scalar_queue(i):
                     ask_at.setdefault(step, []).append(i)
+
+        def lag_of(i):
+            if big_of(i) < 0:
+                return 0
+            return 1 if big_of(i) >= LAST_GATHER_TILE else LAG
 
         done = 0
         for i in range(N_TILES + 4):
@@ -284,15 +315,18 @@ def tile_routed_moe_kernel(tc, xT, w1, w3, w2, gate, offs, pos1, pos2, out):
                 if i == 5:
                     nc.sync.dma_start(pos1_t[:], pos1)
                     nc.sync.dma_start(pos2_t[:], pos2)
-                nxt = i // 4 + 1
-                k = i % 4
+                nxt = big_of(i) // 4 + 1 if big_of(i) >= 0 else E + 1
+                k = big_of(i) % 4
                 if 2 <= nxt <= E and k == 0:
                     quantize_x(nxt - 1)
                 if nxt < E:
                     gather(nxt, k // 2, 2 * (k % 2))
                     gather(nxt, k // 2, 2 * (k % 2) + 1)
-            lag = min(LAG, max(0, N_TILES - 1 - i))
-            while done < N_TILES and done <= i - lag:
+            if i >= END_FROM:
+                for fn, arg in later.get(i, []):
+                    fn(arg)
+                later[i] = []
+            while done < N_TILES and done + lag_of(done) <= i:
                 unit_done(done, i)
                 done += 1
             for fn, arg in later.get(i, []):

@@ -25,7 +25,7 @@ TILE = PACK * H
 RAW_BUFS = 7
 GRP_BUFS = 4
 LAG = 2
-AHEAD = 11
+AHEAD = 7
 BIG_TILES = 4 * E
 W2_GROUPS = [(0, 4), (4, 2), (6, 1), (7, 1)]
 W2_TILES = [(0, 2), (2, 2), (4, 2), (6, 1), (7, 1)]
@@ -132,7 +132,7 @@ def tile_routed_moe_kernel(tc, xT, w1, w3, w2, gate, offs, pos1, pos2, out):
             b = big_of(i)
             return b >= 0 and b % 2 == 1 and b >= 12
 
-        def load_big(i):
+        def load(i):
             kind, e, g = tile_info(i)
             if scalar_interleaves(i):
                 raw = raws_s.tile([P, TILE], F32, name="raw_s")
@@ -140,27 +140,42 @@ def tile_routed_moe_kernel(tc, xT, w1, w3, w2, gate, offs, pos1, pos2, out):
                 raw = raws_v.tile([P, TILE], F32, name="raw_v")
             else:
                 raw = raws.tile([P, TILE], F32, name="raw")
-            w = w1 if kind == "w1" else w3
-            queue = nc.scalar if on_scalar_queue(i) else nc.sync
-            queue.dma_start(
-                out=raw[:].rearrange("p (j c) -> p j c", j=PACK),
-                in_=w[e, g * K_PASS : (g + 1) * K_PASS, :].rearrange("(p j) c -> p j c", j=PACK),
-            )
             raw_of[i] = raw
+            if kind == "w2":
+                e0, count = W2_TILES[e]
+                nc.sync.dma_start(
+                    out=raw[:, 0 : count * PACK * N].rearrange("p (e r) -> p e r", e=count),
+                    in_=w2[e0 : e0 + count].rearrange("e (p j) n -> p e (j n)", j=PACK),
+                )
+            else:
+                w = w1 if kind == "w1" else w3
+                queue = nc.scalar if on_scalar_queue(i) else nc.sync
+                queue.dma_start(
+                    out=raw[:].rearrange("p (j c) -> p j c", j=PACK),
+                    in_=w[e, g * K_PASS : (g + 1) * K_PASS, :].rearrange("(p j) c -> p j c", j=PACK),
+                )
+            if i == 5:
+                nc.sync.dma_start(pos1_t[:], pos1)
+                nc.sync.dma_start(pos2_t[:], pos2)
+            if i == N_TILES - 1:
+                for nb in range(NB):
+                    nc.sync.dma_start(gate_tiles[nb][:], gate[:, nb * P : (nb + 1) * P, :].rearrange("r p t -> p r t"))
+
+        freed_at = {}
+        for ring_depth, tenants in ((3, [i for i in range(N_TILES) if scalar_interleaves(i)]),
+                                    (3, [i for i in range(N_TILES) if tile_info(i)[0] == "w3" and not scalar_interleaves(i)]),
+                                    (RAW_BUFS, [-1, -1] + [i for i in range(N_TILES) if tile_info(i)[0] != "w3"])):
+            for k, i in enumerate(tenants):
+                freed_at[i] = tenants[k - ring_depth] if k >= ring_depth else -1
+
+        def load_up_to(step):
+            while len(raw_of) < N_TILES and len(raw_of) - AHEAD <= step and freed_at[len(raw_of)] <= step:
+                load(len(raw_of))
 
         def load_and_interleave(i):
             kind, e, g = tile_info(i)
             on_scalar = scalar_interleaves(i)
-            if kind != "w2":
-                if i not in raw_of:
-                    load_big(i)
-                raw = raw_of[i]
-            elif on_scalar:
-                raw = raws_s.tile([P, TILE], F32, name="raw_s")
-            elif kind == "w3":
-                raw = raws_v.tile([P, TILE], F32, name="raw_v")
-            else:
-                raw = raws.tile([P, TILE], F32, name="raw")
+            raw = raw_of[i]
             if kind == "w2":
                 e0, count = W2_TILES[e]
                 a = w2_group_of(e0)
@@ -168,10 +183,6 @@ def tile_routed_moe_kernel(tc, xT, w1, w3, w2, gate, offs, pos1, pos2, out):
                 if first == 0:
                     grouped[("w2", a)] = stage.tile([P, PASSES * TILE], BF16, name="grp", align_bytes=64)
                 width = count * PACK * N
-                nc.sync.dma_start(
-                    out=raw[:, 0:width].rearrange("p (e r) -> p e r", e=count),
-                    in_=w2[e0 : e0 + count].rearrange("e (p j) n -> p e (j n)", j=PACK),
-                )
                 dst = grouped[("w2", a)][:, first * PACK * N : first * PACK * N + width].rearrange("p (e n j) -> p e n j", e=count, j=PACK)
                 src = raw[:, 0:width].rearrange("p (e j n) -> p e n j", e=count, j=PACK)
                 share = W2_SCALAR_COLS
@@ -264,6 +275,7 @@ def tile_routed_moe_kernel(tc, xT, w1, w3, w2, gate, offs, pos1, pos2, out):
             if halves_ready[a] == 2:
                 layer2(a)
 
+        load_up_to(-1)
         for g in range(PASSES):
             for t in range(PACK):
                 gather(0, g, t)
@@ -292,15 +304,6 @@ def tile_routed_moe_kernel(tc, xT, w1, w3, w2, gate, offs, pos1, pos2, out):
                         defer(step + 2, quantize_hidden, a)
                         defer(step + 2, second_layer_if_ready, a)
 
-        ask_at = {}
-        for ring_depth, tenants in ((3, [i for i in range(N_TILES) if scalar_interleaves(i)]),
-                                    (3, [i for i in range(N_TILES) if big_of(i) % 2 == 1 and big_of(i) >= 0 and not scalar_interleaves(i)])):
-            step = 0
-            for k, i in enumerate(tenants):
-                step = max(step, i - AHEAD, tenants[k - ring_depth] + 1) if on_scalar_queue(i) else i
-                if on_scalar_queue(i):
-                    ask_at.setdefault(step, []).append(i)
-
         def lag_of(i):
             if big_of(i) < 0:
                 return 0
@@ -310,11 +313,7 @@ def tile_routed_moe_kernel(tc, xT, w1, w3, w2, gate, offs, pos1, pos2, out):
         for i in range(N_TILES + 4):
             if i < N_TILES:
                 load_and_interleave(i)
-                for ahead in ask_at.get(i, []):
-                    load_big(ahead)
-                if i == 5:
-                    nc.sync.dma_start(pos1_t[:], pos1)
-                    nc.sync.dma_start(pos2_t[:], pos2)
+                load_up_to(i)
                 nxt = big_of(i) // 4 + 1 if big_of(i) >= 0 else E + 1
                 k = big_of(i) % 4
                 if 2 <= nxt <= E and k == 0:
@@ -331,9 +330,6 @@ def tile_routed_moe_kernel(tc, xT, w1, w3, w2, gate, offs, pos1, pos2, out):
                 done += 1
             for fn, arg in later.get(i, []):
                 fn(arg)
-
-        for nb in range(NB):
-            nc.sync.dma_start(gate_tiles[nb][:], gate[:, nb * P : (nb + 1) * P, :].rearrange("r p t -> p r t"))
 
         weighted = {}
 

@@ -75,10 +75,7 @@ def tile_routed_moe_kernel(tc, xT, w1, w3, w2, gate, offs, pos1, pos2, out):
         x_bf = []
         for g in range(PASSES):
             x_raw = raws.tile([P, TILE], F32, name="raw")
-            nc.sync.dma_start(
-                out=x_raw[:].rearrange("p (t n) -> p t n", t=PACK),
-                in_=xT[g * K_PASS : (g + 1) * K_PASS, :].rearrange("(p t) n -> p t n", t=PACK),
-            )
+            nc.sync.dma_start(out=x_raw[:], in_=xT[g * K_PASS : (g + 1) * K_PASS, :].rearrange("(p t) n -> p (t n)", t=PACK))
             planes = keep.tile([P, PACK, T], BF16, name="x_bf%d" % g)
             nc.vector.tensor_copy(out=planes[:].rearrange("p t n -> p (t n)"), in_=x_raw[:])
             x_bf.append(planes)
@@ -150,10 +147,7 @@ def tile_routed_moe_kernel(tc, xT, w1, w3, w2, gate, offs, pos1, pos2, out):
             else:
                 w = w1 if kind == "w1" else w3
                 queue = nc.scalar if on_scalar_queue(i) else nc.sync
-                queue.dma_start(
-                    out=raw[:].rearrange("p (j c) -> p j c", j=PACK),
-                    in_=w[e, g * K_PASS : (g + 1) * K_PASS, :].rearrange("(p j) c -> p j c", j=PACK),
-                )
+                queue.dma_start(out=raw[:], in_=w[e, g * K_PASS : (g + 1) * K_PASS, :].rearrange("(p j) c -> p (j c)", j=PACK))
             if i == 5:
                 nc.sync.dma_start(pos1_t[:], pos1)
                 nc.sync.dma_start(pos2_t[:], pos2)

@@ -25,7 +25,7 @@ TILE = PACK * H
 RAW_BUFS = 7
 GRP_BUFS = 4
 LAG = 2
-AHEAD = 7
+AHEAD = 8
 BIG_TILES = 4 * E
 W2_GROUPS = [(0, 4), (4, 2), (6, 1), (7, 1)]
 W2_TILES = [(0, 2), (2, 2), (4, 2), (6, 1), (7, 1)]

@@ -326,21 +326,31 @@ def tile_routed_moe_kernel(tc, xT, w1, w3, w2, gate, offs, pos1, pos2, out):
                 fn(arg)
 
         weighted = {}
+        HALF = T // 2
 
-        def fetch(nb, r):
-            weighted[(nb, r)] = hid.tile([P, T], F32, name="weighted%d" % r, bufs=2)
+        def fetch(nb, r, cols=slice(0, T)):
+            if cols.start == 0:
+                weighted[(nb, r)] = hid.tile([P, T], F32, name="weighted%d" % r, bufs=2)
             nc.vector.tensor_tensor(
-                weighted[(nb, r)][:], y_tiles[nb][:].indirect((pos1_t, pos2_t)[r][:]), gate_tiles[nb][:, r, :], MULT
+                weighted[(nb, r)][:, cols],
+                y_tiles[nb][:].indirect((pos1_t, pos2_t)[r][:, cols.start // 16 : cols.stop // 16]),
+                gate_tiles[nb][:, r, cols],
+                MULT,
             )
 
-        def add_and_store(nb):
-            total = hid.tile([P, T], F32, name="total")
-            nc.vector.tensor_tensor(total[:], weighted[(nb, 0)][:], weighted[(nb, 1)][:], ADD)
-            nc.sync.dma_start(out[nb * P : (nb + 1) * P, :], total[:])
+        totals = {}
+
+        def add_and_store(nb, cols=slice(0, T)):
+            if cols.start == 0:
+                totals[nb] = hid.tile([P, T], F32, name="total")
+            nc.vector.tensor_tensor(totals[nb][:, cols], weighted[(nb, 0)][:, cols], weighted[(nb, 1)][:, cols], ADD)
+            nc.sync.dma_start(out[nb * P : (nb + 1) * P, cols], totals[nb][:, cols])
 
         fetch(0, 0)
         fetch(0, 1)
         fetch(1, 0)
         add_and_store(0)
-        fetch(1, 1)
-        add_and_store(1)
+        fetch(1, 1, slice(0, HALF))
+        fetch(1, 1, slice(HALF, T))
+        add_and_store(1, slice(0, HALF))
+        add_and_store(1, slice(HALF, T))

@@ -177,11 +177,11 @@ def tile_routed_moe_kernel(tc, xT, w1, w3, w2, gate, offs, pos1, pos2, out):
                 if first == 0:
                     grouped[("w2", a)] = stage.tile([P, PASSES * TILE], BF16, name="grp", align_bytes=64)
                 width = count * PACK * N
-                dst = grouped[("w2", a)][:, first * PACK * N : first * PACK * N + width].rearrange("p (e n j) -> p e n j", e=count, j=PACK)
-                src = raw[:, 0:width].rearrange("p (e j n) -> p e n j", e=count, j=PACK)
-                share = W2_SCALAR_COLS
-                nc.scalar.copy(out=dst[:, :, 0:share, :], in_=src[:, :, 0:share, :])
-                nc.vector.tensor_copy(out=dst[:, :, share:, :], in_=src[:, :, share:, :])
+                dst = grouped[("w2", a)][:, first * PACK * N : first * PACK * N + width].rearrange("p (e c i j) -> p e c j i", e=count, i=4, j=PACK)
+                src = raw[:, 0:width].rearrange("p (e j c i) -> p e c j i", e=count, j=PACK, i=4)
+                share = W2_SCALAR_COLS // 4
+                nc.scalar.copy(out=dst[:, :, 0:share], in_=src[:, :, 0:share])
+                nc.vector.tensor_copy(out=dst[:, :, share:], in_=src[:, :, share:])
             else:
                 if g == 0:
                     grouped[(kind, e)] = stage.tile([P, PASSES * TILE], BF16, name="grp", align_bytes=64)

@@ -228,9 +228,9 @@ def tile_routed_moe_kernel(tc, xT, w1, w3, w2, gate, offs, pos1, pos2, out):
 
         def gate_hidden(e):
             nc.vector.tensor_tensor(
-                h_bf[:, e, :, :],
-                hidden[e][:].rearrange("p t n -> p n t"),
-                banks[("w3", e)][:].rearrange("p t n -> p n t"),
+                h_bf[:, e, :, :].rearrange("p (c i) t -> p c t i", i=4),
+                hidden[e][:].rearrange("p t (c i) -> p c t i", i=4),
+                banks[("w3", e)][:].rearrange("p t (c i) -> p c t i", i=4),
                 MULT,
             )
 

@@ -23,6 +23,7 @@ PASSES = K // K_PASS
 NB = N // P
 TILE = PACK * H
 RAW_BUFS = 7
+DMA_ALIGN = 256
 GRP_BUFS = 4
 LAG = 2
 AHEAD = 8
@@ -74,7 +75,7 @@ def tile_routed_moe_kernel(tc, xT, w1, w3, w2, gate, offs, pos1, pos2, out):
 
         x_bf = []
         for g in range(PASSES):
-            x_raw = raws.tile([P, TILE], F32, name="raw")
+            x_raw = raws.tile([P, TILE], F32, name="raw", align_bytes=DMA_ALIGN)
             nc.sync.dma_start(out=x_raw[:], in_=xT[g * K_PASS : (g + 1) * K_PASS, :].rearrange("(p t) n -> p (t n)", t=PACK))
             planes = keep.tile([P, PACK, T], BF16, name="x_bf%d" % g)
             nc.vector.tensor_copy(out=planes[:].rearrange("p t n -> p (t n)"), in_=x_raw[:])
@@ -86,7 +87,7 @@ def tile_routed_moe_kernel(tc, xT, w1, w3, w2, gate, offs, pos1, pos2, out):
         h_scales = keep.tile([P, E, C], U8, name="h_scales", align_bytes=64)
         h_bf = keep.tile([P, E, C, PACK], BF16, name="h_bf", align_bytes=64)
         y_tiles = [keep.tile([P, E * C], F32, name="y%d" % nb) for nb in range(NB)]
-        gate_tiles = [keep.tile([P, 2, T], F32, name="gate%d" % nb) for nb in range(NB)]
+        gate_tiles = [keep.tile([P, 2, T], F32, name="gate%d" % nb, align_bytes=DMA_ALIGN) for nb in range(NB)]
 
         gathered = {}
 
@@ -132,11 +133,11 @@ def tile_routed_moe_kernel(tc, xT, w1, w3, w2, gate, offs, pos1, pos2, out):
         def load(i):
             kind, e, g = tile_info(i)
             if scalar_interleaves(i):
-                raw = raws_s.tile([P, TILE], F32, name="raw_s")
+                raw = raws_s.tile([P, TILE], F32, name="raw_s", align_bytes=DMA_ALIGN)
             elif kind == "w3":
-                raw = raws_v.tile([P, TILE], F32, name="raw_v")
+                raw = raws_v.tile([P, TILE], F32, name="raw_v", align_bytes=DMA_ALIGN)
             else:
-                raw = raws.tile([P, TILE], F32, name="raw")
+                raw = raws.tile([P, TILE], F32, name="raw", align_bytes=DMA_ALIGN)
             raw_of[i] = raw
             if kind == "w2":
                 e0, count = W2_TILES[e]

@@ -77,23 +77,23 @@ def tile_routed_moe_kernel(tc, xT, w1, w3, w2, gate, offs, pos1, pos2, out):
         for g in range(PASSES):
             x_raw = raws.tile([P, TILE], F32, name="raw", align_bytes=DMA_ALIGN)
             nc.sync.dma_start(out=x_raw[:], in_=xT[g * K_PASS : (g + 1) * K_PASS, :].rearrange("(p t) n -> p (t n)", t=PACK))
-            planes = keep.tile([P, PACK, T], BF16, name="x_bf%d" % g)
+            planes = keep.tile([P, PACK, T], BF16, name="x_bf%d" % g, align_bytes=DMA_ALIGN)
             nc.vector.tensor_copy(out=planes[:].rearrange("p t n -> p (t n)"), in_=x_raw[:])
             x_bf.append(planes)
 
-        x_codes = keep.tile([P, E, PASSES, C], U32, name="x_codes", align_bytes=64)
-        x_scales = keep.tile([P, E, PASSES, C], U8, name="x_scales", align_bytes=64)
-        h_codes = keep.tile([P, E, C], U32, name="h_codes", align_bytes=64)
-        h_scales = keep.tile([P, E, C], U8, name="h_scales", align_bytes=64)
-        h_bf = keep.tile([P, E, C, PACK], BF16, name="h_bf", align_bytes=64)
-        y_tiles = [keep.tile([P, E * C], F32, name="y%d" % nb) for nb in range(NB)]
+        x_codes = keep.tile([P, E, PASSES, C], U32, name="x_codes", align_bytes=DMA_ALIGN)
+        x_scales = keep.tile([P, E, PASSES, C], U8, name="x_scales", align_bytes=DMA_ALIGN)
+        h_codes = keep.tile([P, E, C], U32, name="h_codes", align_bytes=DMA_ALIGN)
+        h_scales = keep.tile([P, E, C], U8, name="h_scales", align_bytes=DMA_ALIGN)
+        h_bf = keep.tile([P, E, C, PACK], BF16, name="h_bf", align_bytes=DMA_ALIGN)
+        y_tiles = [keep.tile([P, E * C], F32, name="y%d" % nb, align_bytes=DMA_ALIGN) for nb in range(NB)]
         gate_tiles = [keep.tile([P, 2, T], F32, name="gate%d" % nb, align_bytes=DMA_ALIGN) for nb in range(NB)]
 
         gathered = {}
 
         def gather(e, g, t):
             if g == 0 and t == 0:
-                gathered[e] = stage.tile([P, PASSES, C, PACK], BF16, name="xb", bufs=2, align_bytes=64)
+                gathered[e] = stage.tile([P, PASSES, C, PACK], BF16, name="xb", bufs=2, align_bytes=DMA_ALIGN)
             nc.scalar.activation(
                 out=gathered[e][:, g, :, t],
                 in_=x_bf[g][:, t, :].indirect(offs_t[:, e * C // 16 : (e + 1) * C // 16]),
@@ -176,7 +176,7 @@ def tile_routed_moe_kernel(tc, xT, w1, w3, w2, gate, offs, pos1, pos2, out):
                 a = w2_group_of(e0)
                 first = e0 - W2_GROUPS[a][0]
                 if first == 0:
-                    grouped[("w2", a)] = stage.tile([P, PASSES * TILE], BF16, name="grp", align_bytes=64)
+                    grouped[("w2", a)] = stage.tile([P, PASSES * TILE], BF16, name="grp", align_bytes=DMA_ALIGN)
                 width = count * PACK * N
                 dst = grouped[("w2", a)][:, first * PACK * N : first * PACK * N + width].rearrange("p (e c i j) -> p e c j i", e=count, i=4, j=PACK)
                 src = raw[:, 0:width].rearrange("p (e j c i) -> p e c j i", e=count, j=PACK, i=4)
@@ -185,7 +185,7 @@ def tile_routed_moe_kernel(tc, xT, w1, w3, w2, gate, offs, pos1, pos2, out):
                 nc.vector.tensor_copy(out=dst[:, :, share:], in_=src[:, :, share:])
             else:
                 if g == 0:
-                    grouped[(kind, e)] = stage.tile([P, PASSES * TILE], BF16, name="grp", align_bytes=64)
+                    grouped[(kind, e)] = stage.tile([P, PASSES * TILE], BF16, name="grp", align_bytes=DMA_ALIGN)
                 dst = grouped[(kind, e)][:].rearrange("p (t g m j) -> p g m j t", t=4, g=PASSES, j=PACK)[:, g]
                 src = raw[:].rearrange("p (j m t) -> p m j t", j=PACK, t=4)
                 if on_scalar:
@@ -195,8 +195,8 @@ def tile_routed_moe_kernel(tc, xT, w1, w3, w2, gate, offs, pos1, pos2, out):
 
         def quantize_w(kind, e):
             width = W2_GROUPS[e][1] * N if kind == "w2" else PASSES * H
-            w_codes[(kind, e)] = codes.tile([P, PASSES * H], U32, name=kind + "c", align_bytes=64)
-            w_scales[(kind, e)] = codes.tile([P, PASSES * H], U8, name=kind + "s", align_bytes=64)
+            w_codes[(kind, e)] = codes.tile([P, PASSES * H], U32, name=kind + "c", align_bytes=DMA_ALIGN)
+            w_scales[(kind, e)] = codes.tile([P, PASSES * H], U8, name=kind + "s", align_bytes=DMA_ALIGN)
             nc.vector.quantize_mx(
                 out=w_codes[(kind, e)][:, 0:width].bitcast(FP8X4),
                 scales=w_scales[(kind, e)][:, 0:width],
@@ -223,7 +223,7 @@ def tile_routed_moe_kernel(tc, xT, w1, w3, w2, gate, offs, pos1, pos2, out):
                         )
                 banks[(kind, e)] = bank
                 if kind == "w1":
-                    act = hid.tile([P, PACK, C], F32, name="act")
+                    act = hid.tile([P, PACK, C], F32, name="act", align_bytes=DMA_ALIGN)
                     nc.scalar.activation(out=act[:], in_=bank[:], func=GELU)
                     hidden[e] = act
 
@@ -331,7 +331,7 @@ def tile_routed_moe_kernel(tc, xT, w1, w3, w2, gate, offs, pos1, pos2, out):
 
         def fetch(nb, r, cols=slice(0, T)):
             if cols.start == 0:
-                weighted[(nb, r)] = hid.tile([P, T], F32, name="weighted%d" % r, bufs=2)
+                weighted[(nb, r)] = hid.tile([P, T], F32, name="weighted%d" % r, bufs=2, align_bytes=DMA_ALIGN)
             nc.vector.tensor_tensor(
                 weighted[(nb, r)][:, cols],
                 y_tiles[nb][:].indirect((pos1_t, pos2_t)[r][:, cols.start // 16 : cols.stop // 16]),
@@ -343,7 +343,7 @@ def tile_routed_moe_kernel(tc, xT, w1, w3, w2, gate, offs, pos1, pos2, out):
 
         def add_and_store(nb, cols=slice(0, T)):
             if cols.start == 0:
-                totals[nb] = hid.tile([P, T], F32, name="total")
+                totals[nb] = hid.tile([P, T], F32, name="total", align_bytes=DMA_ALIGN)
             nc.vector.tensor_tensor(totals[nb][:, cols], weighted[(nb, 0)][:, cols], weighted[(nb, 1)][:, cols], ADD)
             nc.sync.dma_start(out[nb * P : (nb + 1) * P, cols], totals[nb][:, cols])
 

@@ -180,9 +180,13 @@ def tile_routed_moe_kernel(tc, xT, w1, w3, w2, gate, offs, pos1, pos2, out):
                 width = count * PACK * N
                 dst = grouped[("w2", a)][:, first * PACK * N : first * PACK * N + width].rearrange("p (e c i j) -> p e c j i", e=count, i=4, j=PACK)
                 src = raw[:, 0:width].rearrange("p (e j c i) -> p e c j i", e=count, j=PACK, i=4)
-                share = W2_SCALAR_COLS // 4
-                nc.scalar.copy(out=dst[:, :, 0:share], in_=src[:, :, 0:share])
-                nc.vector.tensor_copy(out=dst[:, :, share:], in_=src[:, :, share:])
+                if e == len(W2_TILES) - 1:
+                    nc.vector.tensor_copy(out=dst[:, :, 0 : P // 4], in_=src[:, :, 0 : P // 4])
+                    nc.scalar.copy(out=dst[:, :, P // 4 :], in_=src[:, :, P // 4 :])
+                else:
+                    share = W2_SCALAR_COLS // 4
+                    nc.scalar.copy(out=dst[:, :, 0:share], in_=src[:, :, 0:share])
+                    nc.vector.tensor_copy(out=dst[:, :, share:], in_=src[:, :, share:])
             else:
                 if g == 0:
                     grouped[(kind, e)] = stage.tile([P, PASSES * TILE], BF16, name="grp", align_bytes=DMA_ALIGN)
@@ -197,11 +201,14 @@ def tile_routed_moe_kernel(tc, xT, w1, w3, w2, gate, offs, pos1, pos2, out):
             width = W2_GROUPS[e][1] * N if kind == "w2" else PASSES * H
             w_codes[(kind, e)] = codes.tile([P, PASSES * H], U32, name=kind + "c", align_bytes=DMA_ALIGN)
             w_scales[(kind, e)] = codes.tile([P, PASSES * H], U8, name=kind + "s", align_bytes=DMA_ALIGN)
-            nc.vector.quantize_mx(
-                out=w_codes[(kind, e)][:, 0:width].bitcast(FP8X4),
-                scales=w_scales[(kind, e)][:, 0:width],
-                in_=grouped[(kind, e)][:, 0 : PACK * width],
-            )
+            pieces = NB if kind == "w2" and e == len(W2_GROUPS) - 1 else 1
+            for c0 in range(0, width, width // pieces):
+                cols = slice(c0, c0 + width // pieces)
+                nc.vector.quantize_mx(
+                    out=w_codes[(kind, e)][:, cols].bitcast(FP8X4),
+                    scales=w_scales[(kind, e)][:, cols],
+                    in_=grouped[(kind, e)][:, PACK * cols.start : PACK * cols.stop],
+                )
 
         banks = {}
         hidden = {}

@@ -149,10 +149,9 @@ def tile_routed_moe_kernel(tc, xT, w1, w3, w2, gate, offs, pos1, pos2, out):
                 w = w1 if kind == "w1" else w3
                 queue = nc.scalar if on_scalar_queue(i) else nc.sync
                 queue.dma_start(out=raw[:], in_=w[e, g * K_PASS : (g + 1) * K_PASS, :].rearrange("(p j) c -> p (j c)", j=PACK))
-            if i == 5:
+            if i == N_TILES - 1:
                 nc.sync.dma_start(pos1_t[:], pos1)
                 nc.sync.dma_start(pos2_t[:], pos2)
-            if i == N_TILES - 1:
                 for nb in range(NB):
                     nc.sync.dma_start(gate_tiles[nb][:], gate[:, nb * P : (nb + 1) * P, :].rearrange("r p t -> p r t"))
 

@@ -192,7 +192,10 @@ def tile_routed_moe_kernel(tc, xT, w1, w3, w2, gate, offs, pos1, pos2, out):
                 dst = grouped[(kind, e)][:].rearrange("p (t g m j) -> p g m j t", t=4, g=PASSES, j=PACK)[:, g]
                 src = raw[:].rearrange("p (j m t) -> p m j t", j=PACK, t=4)
                 if on_scalar:
-                    nc.scalar.copy(out=dst, in_=src)
+                    nc.scalar.copy(
+                        out=grouped[(kind, e)][:].rearrange("p (t g m a b) -> p g m a t b", t=4, g=PASSES, a=2, b=2)[:, g],
+                        in_=raw[:].rearrange("p (a b m t) -> p m a t b", a=2, b=2, t=4),
+                    )
                 else:
                     nc.vector.tensor_copy(out=dst, in_=src)
 

@@ -91,14 +91,22 @@ def tile_routed_moe_kernel(tc, xT, w1, w3, w2, gate, offs, pos1, pos2, out):
 
         gathered = {}
 
+        pairs = {}
+
         def gather(e, g, t):
             if g == 0 and t == 0:
-                gathered[e] = stage.tile([P, PASSES, C, PACK], BF16, name="xb", bufs=2, align_bytes=DMA_ALIGN)
+                pairs[e] = stage.tile([P, PASSES, 2, C, 2], BF16, name="xp", bufs=2, align_bytes=DMA_ALIGN)
             nc.scalar.activation(
-                out=gathered[e][:, g, :, t],
+                out=pairs[e][:, g, t // 2, :, t % 2],
                 in_=x_bf[g][:, t, :].indirect(offs_t[:, e * C // 16 : (e + 1) * C // 16]),
                 func=COPY,
             )
+            if g == PASSES - 1 and t == PACK - 1:
+                gathered[e] = stage.tile([P, PASSES, C, PACK], BF16, name="xb", bufs=2, align_bytes=DMA_ALIGN)
+                nc.vector.tensor_copy(
+                    out=gathered[e][:].rearrange("p g c (q u) -> p g c q u", q=2),
+                    in_=pairs[e][:].rearrange("p g q c u -> p g c q u"),
+                )
 
         def quantize_x(e):
             nc.vector.quantize_mx(
@@ -340,7 +348,7 @@ def tile_routed_moe_kernel(tc, xT, w1, w3, w2, gate, offs, pos1, pos2, out):
 
         def fetch(nb, r, cols=slice(0, T)):
             if cols.start == 0:
-                weighted[(nb, r)] = hid.tile([P, T], F32, name="weighted%d" % r, bufs=2, align_bytes=DMA_ALIGN)
+                weighted[(nb, r)] = (raws_s, raws_v)[r].tile([P, T], F32, name=("raw_s", "raw_v")[r], align_bytes=DMA_ALIGN)
             nc.vector.tensor_tensor(
                 weighted[(nb, r)][:, cols],
                 y_tiles[nb][:].indirect((pos1_t, pos2_t)[r][:, cols.start // 16 : cols.stop // 16]),

@@ -94,25 +94,25 @@ def tile_routed_moe_kernel(tc, xT, w1, w3, w2, gate, offs, pos1, pos2, out):
         pairs = {}
 
         def gather(e, g, t):
-            if g == 0 and t == 0:
-                pairs[e] = stage.tile([P, PASSES, 2, C, 2], BF16, name="xp", bufs=2, align_bytes=DMA_ALIGN)
+            if e % 2 == 0 and g == 0 and t == 0:
+                pairs[e // 2] = stage.tile([P, 2, PASSES, 2, C, 2], BF16, name="xp", bufs=2, align_bytes=DMA_ALIGN)
             nc.scalar.activation(
-                out=pairs[e][:, g, t // 2, :, t % 2],
+                out=pairs[e // 2][:, e % 2, g, t // 2, :, t % 2],
                 in_=x_bf[g][:, t, :].indirect(offs_t[:, e * C // 16 : (e + 1) * C // 16]),
                 func=COPY,
             )
-            if g == PASSES - 1 and t == PACK - 1:
-                gathered[e] = stage.tile([P, PASSES, C, PACK], BF16, name="xb", bufs=2, align_bytes=DMA_ALIGN)
+            if e % 2 == 1 and g == PASSES - 1 and t == PACK - 1:
+                gathered[e // 2] = stage.tile([P, 2, PASSES, C, PACK], BF16, name="xb", bufs=1, align_bytes=DMA_ALIGN)
                 nc.vector.tensor_copy(
-                    out=gathered[e][:].rearrange("p g c (q u) -> p g c q u", q=2),
-                    in_=pairs[e][:].rearrange("p g q c u -> p g c q u"),
+                    out=gathered[e // 2][:].rearrange("p h g c (q u) -> p (h g) c q u", q=2),
+                    in_=pairs[e // 2][:].rearrange("p h g q c u -> p (h g) c q u"),
                 )
 
         def quantize_x(e):
             nc.vector.quantize_mx(
-                out=x_codes[:, e, :, :].rearrange("p g n -> p (g n)").bitcast(FP8X4),
-                scales=x_scales[:, e, :, :].rearrange("p g n -> p (g n)"),
-                in_=gathered[e][:].rearrange("p g n t -> p (g n t)"),
+                out=x_codes[:, e : e + 2, :, :].rearrange("p e g n -> p (e g n)").bitcast(FP8X4),
+                scales=x_scales[:, e : e + 2, :, :].rearrange("p e g n -> p (e g n)"),
+                in_=gathered[e // 2][:].rearrange("p h g n t -> p (h g n t)"),
             )
 
         def tile_info(i):
@@ -288,9 +288,10 @@ def tile_routed_moe_kernel(tc, xT, w1, w3, w2, gate, offs, pos1, pos2, out):
                 layer2(a)
 
         load_up_to(-1)
-        for g in range(PASSES):
-            for t in range(PACK):
-                gather(0, g, t)
+        for e in range(2):
+            for g in range(PASSES):
+                for t in range(PACK):
+                    gather(e, g, t)
         quantize_x(0)
 
         later = {}
@@ -326,10 +327,10 @@ def tile_routed_moe_kernel(tc, xT, w1, w3, w2, gate, offs, pos1, pos2, out):
             if i < N_TILES:
                 load_and_interleave(i)
                 load_up_to(i)
-                nxt = big_of(i) // 4 + 1 if big_of(i) >= 0 else E + 1
+                nxt = big_of(i) // 4 + 2 if big_of(i) >= 0 else E + 2
                 k = big_of(i) % 4
-                if 2 <= nxt <= E and k == 0:
-                    quantize_x(nxt - 1)
+                if 4 <= nxt <= E and nxt % 2 == 0 and k == 0:
+                    quantize_x(nxt - 2)
                 if nxt < E:
                     gather(nxt, k // 2, 2 * (k % 2))
                     gather(nxt, k // 2, 2 * (k % 2) + 1)

from contextlib import ExitStack

import concourse.mybir as mybir

K, T, E, C, H, N = 1024, 512, 8, 128, 512, 256
FLOPS = 2 * E * C * (2 * K * H + H * N)

F32 = mybir.dt.float32
BF16 = mybir.dt.bfloat16
U32 = mybir.dt.uint32
U16 = mybir.dt.uint16
U8 = mybir.dt.uint8
FP8X4 = mybir.dt.float8_e4m3fn_x4
GELU = mybir.ActivationFunctionType.Gelu_apprx_tanh
COPY = mybir.ActivationFunctionType.Copy
MULT = mybir.AluOpType.mult
ADD = mybir.AluOpType.add

P = 128
PACK = 4
K_PASS = P * PACK
PASSES = K // K_PASS
NB = N // P
TILE = PACK * H
RAW_BUFS = 7
DMA_ALIGN = 256
GRP_BUFS = 4
LAG = 2
AHEAD = 8
BIG_TILES = 4 * E
W2_GROUPS = [(0, 4), (4, 2), (6, 1), (7, 1)]
W2_TILES = [(0, 2), (2, 2), (4, 2), (6, 1), (7, 1)]
W2_AFTER = [31, 31, 31, 31, 31]
N_TILES = BIG_TILES + len(W2_TILES)
END_FROM = BIG_TILES


def load_order():
    order = []
    for big in range(BIG_TILES):
        order.append((("w1", "w3")[big % 2], big // 4, (big % 4) // 2, big))
        for k2, after in enumerate(W2_AFTER):
            if after == big:
                order.append(("w2", k2, 0, -1))
    return order


STREAM = load_order()
W2_SCALAR_COLS = 88
LAST_GATHER_TILE = 4 * (E - 1)


def tile_routed_moe_kernel(tc, xT, w1, w3, w2, gate, offs, pos1, pos2, out):
    nc = tc.nc
    with ExitStack() as ctx:
        lists = ctx.enter_context(tc.tile_pool(name="lists", bufs=1))
        keep = ctx.enter_context(tc.tile_pool(name="keep", bufs=1))
        raws = ctx.enter_context(tc.tile_pool(name="raws", bufs=RAW_BUFS))
        raws_s = ctx.enter_context(tc.tile_pool(name="raws_s", bufs=3))
        raws_v = ctx.enter_context(tc.tile_pool(name="raws_v", bufs=3))
        stage = ctx.enter_context(tc.tile_pool(name="stage", bufs=GRP_BUFS))
        codes = ctx.enter_context(tc.tile_pool(name="codes", bufs=2))
        hid = ctx.enter_context(tc.tile_pool(name="hid", bufs=2))
        psum = ctx.enter_context(tc.psum_pool(name="psum", bufs=2))

        offs_t = lists.tile([P, E * C // 16], U16, name="offs_t")
        pos1_t = lists.tile([P, T // 16], U16, name="pos1_t")
        pos2_t = lists.tile([P, T // 16], U16, name="pos2_t")
        nc.sync.dma_start(offs_t[:], offs)

        warm = keep.tile([P, 1], F32, name="warm")
        warm_out = keep.tile([P, 1], F32, name="warm_out")
        nc.vector.memset(warm[:], 0.0)
        nc.scalar.activation(out=warm_out[:], in_=warm[:], func=GELU)

        x_bf = []
        for g in range(PASSES):
            x_raw = raws.tile([P, TILE], F32, name="raw", align_bytes=DMA_ALIGN)
            nc.sync.dma_start(out=x_raw[:], in_=xT[g * K_PASS : (g + 1) * K_PASS, :].rearrange("(p t) n -> p (t n)", t=PACK))
            planes = keep.tile([P, PACK, T], BF16, name="x_bf%d" % g, align_bytes=DMA_ALIGN)
            nc.vector.tensor_copy(out=planes[:].rearrange("p t n -> p (t n)"), in_=x_raw[:])
            x_bf.append(planes)

        x_codes = keep.tile([P, E, PASSES, C], U32, name="x_codes", align_bytes=DMA_ALIGN)
        x_scales = keep.tile([P, E, PASSES, C], U8, name="x_scales", align_bytes=DMA_ALIGN)
        h_codes = keep.tile([P, E, C], U32, name="h_codes", align_bytes=DMA_ALIGN)
        h_scales = keep.tile([P, E, C], U8, name="h_scales", align_bytes=DMA_ALIGN)
        h_bf = keep.tile([P, E, C, PACK], BF16, name="h_bf", align_bytes=DMA_ALIGN)
        y_tiles = [keep.tile([P, E * C], F32, name="y%d" % nb, align_bytes=DMA_ALIGN) for nb in range(NB)]
        gate_tiles = [keep.tile([P, 2, T], F32, name="gate%d" % nb, align_bytes=DMA_ALIGN) for nb in range(NB)]

        gathered = {}

        pairs = {}

        def gather(e, g, t):
            if e % 2 == 0 and g == 0 and t == 0:
                pairs[e // 2] = stage.tile([P, 2, PASSES, 2, C, 2], BF16, name="xp", bufs=2, align_bytes=DMA_ALIGN)
            nc.scalar.activation(
                out=pairs[e // 2][:, e % 2, g, t // 2, :, t % 2],
                in_=x_bf[g][:, t, :].indirect(offs_t[:, e * C // 16 : (e + 1) * C // 16]),
                func=COPY,
            )
            if e % 2 == 1 and g == PASSES - 1 and t == PACK - 1:
                gathered[e // 2] = stage.tile([P, 2, PASSES, C, PACK], BF16, name="xb", bufs=1, align_bytes=DMA_ALIGN)
                nc.vector.tensor_copy(
                    out=gathered[e // 2][:].rearrange("p h g c (q u) -> p (h g) c q u", q=2),
                    in_=pairs[e // 2][:].rearrange("p h g q c u -> p (h g) c q u"),
                )

        def quantize_x(e):
            nc.vector.quantize_mx(
                out=x_codes[:, e : e + 2, :, :].rearrange("p e g n -> p (e g n)").bitcast(FP8X4),
                scales=x_scales[:, e : e + 2, :, :].rearrange("p e g n -> p (e g n)"),
                in_=gathered[e // 2][:].rearrange("p h g n t -> p (h g n t)"),
            )

        def tile_info(i):
            return STREAM[i][0:3]

        def big_of(i):
            return STREAM[i][3]

        def w2_group_of(e):
            return [a for a, (e0, count) in enumerate(W2_GROUPS) if e0 <= e < e0 + count][0]

        w_codes = {}
        w_scales = {}
        grouped = {}

        raw_of = {}

        def scalar_interleaves(i):
            b = big_of(i)
            return b >= 0 and (b % 4 == 1 or (b >= LAST_GATHER_TILE and b % 4 == 3))

        def on_scalar_queue(i):
            b = big_of(i)
            return b >= 0 and b % 2 == 1 and b >= 12

        def load(i):
            kind, e, g = tile_info(i)
            if scalar_interleaves(i):
                raw = raws_s.tile([P, TILE], F32, name="raw_s", align_bytes=DMA_ALIGN)
            elif kind == "w3":
                raw = raws_v.tile([P, TILE], F32, name="raw_v", align_bytes=DMA_ALIGN)
            else:
                raw = raws.tile([P, TILE], F32, name="raw", align_bytes=DMA_ALIGN)
            raw_of[i] = raw
            if kind == "w2":
                e0, count = W2_TILES[e]
                nc.sync.dma_start(
                    out=raw[:, 0 : count * PACK * N].rearrange("p (e r) -> p e r", e=count),
                    in_=w2[e0 : e0 + count].rearrange("e (p j) n -> p e (j n)", j=PACK),
                )
            else:
                w = w1 if kind == "w1" else w3
                queue = nc.scalar if on_scalar_queue(i) else nc.sync
                queue.dma_start(out=raw[:], in_=w[e, g * K_PASS : (g + 1) * K_PASS, :].rearrange("(p j) c -> p (j c)", j=PACK))
            if i == N_TILES - 1:
                nc.sync.dma_start(pos1_t[:], pos1)
                nc.sync.dma_start(pos2_t[:], pos2)
                for nb in range(NB):
                    nc.sync.dma_start(gate_tiles[nb][:], gate[:, nb * P : (nb + 1) * P, :].rearrange("r p t -> p r t"))

        freed_at = {}
        for ring_depth, tenants in ((3, [i for i in range(N_TILES) if scalar_interleaves(i)]),
                                    (3, [i for i in range(N_TILES) if tile_info(i)[0] == "w3" and not scalar_interleaves(i)]),
                                    (RAW_BUFS, [-1, -1] + [i for i in range(N_TILES) if tile_info(i)[0] != "w3"])):
            for k, i in enumerate(tenants):
                freed_at[i] = tenants[k - ring_depth] if k >= ring_depth else -1

        def load_up_to(step):
            while len(raw_of) < N_TILES and len(raw_of) - AHEAD <= step and freed_at[len(raw_of)] <= step:
                load(len(raw_of))

        def load_and_interleave(i):
            kind, e, g = tile_info(i)
            on_scalar = scalar_interleaves(i)
            raw = raw_of[i]
            if kind == "w2":
                e0, count = W2_TILES[e]
                a = w2_group_of(e0)
                first = e0 - W2_GROUPS[a][0]
                if first == 0:
                    grouped[("w2", a)] = stage.tile([P, PASSES * TILE], BF16, name="grp", align_bytes=DMA_ALIGN)
                width = count * PACK * N
                dst = grouped[("w2", a)][:, first * PACK * N : first * PACK * N + width].rearrange("p (e c i j) -> p e c j i", e=count, i=4, j=PACK)
                src = raw[:, 0:width].rearrange("p (e j c i) -> p e c j i", e=count, j=PACK, i=4)
                if e == len(W2_TILES) - 1:
                    nc.vector.tensor_copy(out=dst[:, :, 0 : P // 4], in_=src[:, :, 0 : P // 4])
                    nc.scalar.copy(out=dst[:, :, P // 4 :], in_=src[:, :, P // 4 :])
                else:
                    share = W2_SCALAR_COLS // 4
                    nc.scalar.copy(out=dst[:, :, 0:share], in_=src[:, :, 0:share])
                    nc.vector.tensor_copy(out=dst[:, :, share:], in_=src[:, :, share:])
            else:
                if g == 0:
                    grouped[(kind, e)] = stage.tile([P, PASSES * TILE], BF16, name="grp", align_bytes=DMA_ALIGN)
                dst = grouped[(kind, e)][:].rearrange("p (t g m j) -> p g m j t", t=4, g=PASSES, j=PACK)[:, g]
                src = raw[:].rearrange("p (j m t) -> p m j t", j=PACK, t=4)
                if on_scalar:
                    nc.scalar.copy(
                        out=grouped[(kind, e)][:].rearrange("p (t g m a b) -> p g m a t b", t=4, g=PASSES, a=2, b=2)[:, g],
                        in_=raw[:].rearrange("p (a b m t) -> p m a t b", a=2, b=2, t=4),
                    )
                else:
                    nc.vector.tensor_copy(out=dst, in_=src)

        def quantize_w(kind, e):
            width = W2_GROUPS[e][1] * N if kind == "w2" else PASSES * H
            w_codes[(kind, e)] = codes.tile([P, PASSES * H], U32, name=kind + "c", align_bytes=DMA_ALIGN)
            w_scales[(kind, e)] = codes.tile([P, PASSES * H], U8, name=kind + "s", align_bytes=DMA_ALIGN)
            pieces = NB if kind == "w2" and e == len(W2_GROUPS) - 1 else 1
            for c0 in range(0, width, width // pieces):
                cols = slice(c0, c0 + width // pieces)
                nc.vector.quantize_mx(
                    out=w_codes[(kind, e)][:, cols].bitcast(FP8X4),
                    scales=w_scales[(kind, e)][:, cols],
                    in_=grouped[(kind, e)][:, PACK * cols.start : PACK * cols.stop],
                )

        banks = {}
        hidden = {}

        def layer1(e):
            for kind in ("w1", "w3"):
                bank = psum.tile([P, PACK, C], F32, name="bank_" + kind)
                for t in range(PACK):
                    for g in range(PASSES):
                        cols = slice((t * PASSES + g) * P, (t * PASSES + g + 1) * P)
                        nc.tensor.matmul_mx(
                            out=bank[:, t, :],
                            lhsT=w_codes[(kind, e)][:, cols].bitcast(FP8X4),
                            lhsT_scale=w_scales[(kind, e)][:, cols],
                            rhs=x_codes[:, e, g, :].bitcast(FP8X4),
                            rhs_scale=x_scales[:, e, g, :],
                            start=(g == 0),
                            stop=(g == PASSES - 1),
                        )
                banks[(kind, e)] = bank
                if kind == "w1":
                    act = hid.tile([P, PACK, C], F32, name="act", align_bytes=DMA_ALIGN)
                    nc.scalar.activation(out=act[:], in_=bank[:], func=GELU)
                    hidden[e] = act

        def gate_hidden(e):
            nc.vector.tensor_tensor(
                h_bf[:, e, :, :].rearrange("p (c i) t -> p c t i", i=4),
                hidden[e][:].rearrange("p t (c i) -> p c t i", i=4),
                banks[("w3", e)][:].rearrange("p t (c i) -> p c t i", i=4),
                MULT,
            )

        def quantize_hidden(a):
            e0, count = W2_GROUPS[a]
            nc.vector.quantize_mx(
                out=h_codes[:, e0 : e0 + count, :].rearrange("p e n -> p (e n)").bitcast(FP8X4),
                scales=h_scales[:, e0 : e0 + count, :].rearrange("p e n -> p (e n)"),
                in_=h_bf[:, e0 : e0 + count, :, :].rearrange("p e n t -> p (e n t)"),
            )

        def layer2(a):
            e0, count = W2_GROUPS[a]
            for nb in range(NB):
                bank = psum.tile([P, PACK, C], F32, name="bank_y", bufs=3)
                for k in range(count):
                    cols = slice(k * N + nb * P, k * N + (nb + 1) * P)
                    nc.tensor.matmul_mx(
                        out=bank[:, k, :],
                        lhsT=w_codes[("w2", a)][:, cols].bitcast(FP8X4),
                        lhsT_scale=w_scales[("w2", a)][:, cols],
                        rhs=h_codes[:, e0 + k, :].bitcast(FP8X4),
                        rhs_scale=h_scales[:, e0 + k, :],
                        start=True,
                        stop=True,
                    )
                nc.scalar.copy(
                    out=y_tiles[nb][:, e0 * C : (e0 + count) * C],
                    in_=bank[:, 0:count, :].rearrange("p k c -> p (k c)"),
                )

        halves_ready = {}

        def second_layer_if_ready(a):
            halves_ready[a] = halves_ready.get(a, 0) + 1
            if halves_ready[a] == 2:
                layer2(a)

        load_up_to(-1)
        for e in range(2):
            for g in range(PASSES):
                for t in range(PACK):
                    gather(e, g, t)
        quantize_x(0)

        later = {}

        def defer(step, fn, arg):
            later.setdefault(step, []).append((fn, arg))

        def unit_done(i, step):
            kind, e, g = tile_info(i)
            if kind == "w2":
                e0, count = W2_TILES[e]
                a = w2_group_of(e0)
                if e0 + count == W2_GROUPS[a][0] + W2_GROUPS[a][1]:
                    quantize_w("w2", a)
                    defer(step, second_layer_if_ready, a)
            elif g == PASSES - 1:
                quantize_w(kind, e)
                if kind == "w3":
                    defer(step, layer1, e)
                    defer(step + 1, gate_hidden, e)
                    a = w2_group_of(e)
                    if e == W2_GROUPS[a][0] + W2_GROUPS[a][1] - 1:
                        defer(step + 2, quantize_hidden, a)
                        defer(step + 2, second_layer_if_ready, a)

        def lag_of(i):
            if big_of(i) < 0:
                return 0
            return 1 if big_of(i) >= LAST_GATHER_TILE else LAG

        done = 0
        for i in range(N_TILES + 4):
            if i < N_TILES:
                load_and_interleave(i)
                load_up_to(i)
                nxt = big_of(i) // 4 + 2 if big_of(i) >= 0 else E + 2
                k = big_of(i) % 4
                if 4 <= nxt <= E and nxt % 2 == 0 and k == 0:
                    quantize_x(nxt - 2)
                if nxt < E:
                    gather(nxt, k // 2, 2 * (k % 2))
                    gather(nxt, k // 2, 2 * (k % 2) + 1)
            if i >= END_FROM:
                for fn, arg in later.get(i, []):
                    fn(arg)
                later[i] = []
            while done < N_TILES and done + lag_of(done) <= i:
                unit_done(done, i)
                done += 1
            for fn, arg in later.get(i, []):
                fn(arg)

        weighted = {}
        HALF = T // 2

        def fetch(nb, r, cols=slice(0, T)):
            if cols.start == 0:
                weighted[(nb, r)] = (raws_s, raws_v)[r].tile([P, T], F32, name=("raw_s", "raw_v")[r], align_bytes=DMA_ALIGN)
            nc.vector.tensor_tensor(
                weighted[(nb, r)][:, cols],
                y_tiles[nb][:].indirect((pos1_t, pos2_t)[r][:, cols.start // 16 : cols.stop // 16]),
                gate_tiles[nb][:, r, cols],
                MULT,
            )

        totals = {}

        def add_and_store(nb, cols=slice(0, T)):
            if cols.start == 0:
                totals[nb] = hid.tile([P, T], F32, name="total", align_bytes=DMA_ALIGN)
            nc.vector.tensor_tensor(totals[nb][:, cols], weighted[(nb, 0)][:, cols], weighted[(nb, 1)][:, cols], ADD)
            nc.sync.dma_start(out[nb * P : (nb + 1) * P, cols], totals[nb][:, cols])

        fetch(0, 0)
        fetch(0, 1)
        fetch(1, 0)
        add_and_store(0)
        fetch(1, 1, slice(0, HALF))
        fetch(1, 1, slice(HALF, T))
        add_and_store(1, slice(0, HALF))
        add_and_store(1, slice(HALF, T))
